import numpy as np
import ml_dtypes


def mxq(x, axis, fmt="e4m3"):
    dtype, down = {"e4m3": (ml_dtypes.float8_e4m3fn, 7), "e5m2": (ml_dtypes.float8_e5m2, 14)}[fmt]
    v = np.moveaxis(np.asarray(x, np.float32).astype(ml_dtypes.bfloat16).astype(np.float64), axis, -1)
    blocks = v.reshape(v.shape[:-1] + (-1, 32))
    amax = np.abs(blocks).max(-1, keepdims=True)
    byte = np.maximum(np.where(amax > 0, np.frexp(amax)[1] - 1 + 127, 0) - down, 1)
    scale = np.exp2(byte - 127.0)
    codes = (blocks / scale).astype(np.float32).astype(dtype).astype(np.float64)
    return np.moveaxis((codes * scale).reshape(v.shape), -1, axis)


WIDE = False


def mx_kscale(k):
    if not WIDE:
        return np.ones(k)
    levels = np.array([10, -10, 5, -5, 0])
    if k % 512:
        return np.exp2(np.random.permutation(np.resize(levels, k // 32))).repeat(32)
    a = np.empty((k // 512, 16))
    for p in range(k // 512):
        a[p, :8] = np.random.permutation(np.resize(levels, 8))
        for g in range(8):
            far = levels[np.abs(levels - a[p, g]) >= 10]
            a[p, g + 8] = far[np.random.randint(len(far))]
    return np.exp2(a.ravel()).repeat(32)


def f64(x):
    return np.asarray(x).astype(np.float64)


def striped(idx):
    return np.tile(idx.reshape(-1, 16).T, (8, 1)).astype(np.uint16)


def unstriped(offs):
    return offs[:16].T.reshape(-1).astype(np.int64)


def pack_weight(w):
    k, n = w.shape
    w = f64(np.asarray(w, np.float32).astype(ml_dtypes.bfloat16)).reshape(k // 32, 32, n)
    amax = np.abs(w).max(1)
    byte = np.clip(np.where(amax > 0, np.frexp(amax)[1] - 1 + 127 - 7, 1), 1, 254)
    scaled = (w * np.exp2(127.0 - byte)[:, None, :]).reshape(k, n).astype(np.float32)
    words = np.ascontiguousarray(scaled.reshape(k // 512, 128, 4, n).transpose(0, 1, 3, 2)).astype(ml_dtypes.float8_e4m3fn).view(np.uint8)
    return words, np.ascontiguousarray(byte.astype(np.uint8).reshape(k // 512, 16, n))


def unpack_weight(words, scales):
    g, p, n, _ = words.shape
    vals = np.ascontiguousarray(words).view(ml_dtypes.float8_e4m3fn).astype(np.float64) * np.repeat(np.exp2(scales.astype(np.float64) - 127.0), 8, axis=1)[..., None]
    return vals.transpose(0, 1, 3, 2).reshape(g * 512, n)


K, T, S, N = 512, 4096, 1024, 128


def setup_inputs():
    n = np.random.standard_normal
    s = mx_kscale(K)[:, None]
    w1, w2 = n((2, K, N)) / np.sqrt(2 * K) / s[None]
    p1, p2 = pack_weight(w1), pack_weight(w2)
    return {
        "xT": (n((K, S)) * s).astype(np.float32),
        "sT": (n((K, T)) * s).astype(np.float32),
        "w1_words": p1[0],
        "w1_scales": p1[1],
        "w2_words": p2[0],
        "w2_scales": p2[1],
        "offs": striped(np.random.permutation(T)[:S]),
    }


def reference(xT, sT, w1_words, w1_scales, w2_words, w2_scales, offs):
    y = unpack_weight(w1_words, w1_scales).T @ mxq(f64(xT), 0, "e4m3") + unpack_weight(w2_words, w2_scales).T @ mxq(f64(sT)[:, unstriped(offs)], 0, "e4m3")
    return y

@@ -1,0 +1,166 @@
+from contextlib import ExitStack
+
+import concourse.mybir as mybir
+
+F32 = mybir.dt.float32
+BF16 = mybir.dt.bfloat16
+I32 = mybir.dt.int32
+U32 = mybir.dt.uint32
+U16 = mybir.dt.uint16
+U8 = mybir.dt.uint8
+FP8X4 = mybir.dt.float8_e4m3fn_x4
+
+P = 128
+PACK = 4
+T = 4096
+S = 1024
+M = 128
+LISTED = 16
+LOAD = 256
+BLOCKS = ((0, 256), (256, 256), (512, 256), (768, 128), (896, 128))
+
+FLOPS = 2 * 2 * 512 * M * S
+
+
+def tile_picked_recall_none_e_kernel(
+    tc, xT, sT, w1_words, w1_scales, w2_words, w2_scales, offs, out
+):
+    nc = tc.nc
+    with ExitStack() as ctx:
+        keep = ctx.enter_context(tc.tile_pool(name="keep", bufs=1))
+        psum = ctx.enter_context(tc.psum_pool(name="psum", bufs=1))
+
+        s_rows = sT.rearrange("(p t) n -> p t n", t=PACK)
+        x_rows = xT.rearrange("(p t) n -> p t n", t=PACK)
+
+        planes = [keep.tile([P, T], F32, name=f"plane{t}") for t in range(PACK)]
+        offsets = keep.tile([P, S // LISTED], U16, name="offsets")
+        w_codes = [keep.tile([P, M], U32, name=f"w_codes{i}", align_bytes=64) for i in range(2)]
+        w_scales = [keep.tile([P, M], U8, name=f"w_scales{i}", align_bytes=64) for i in range(2)]
+        x_raw = [keep.tile([P, PACK, LOAD], F32, name=f"x_raw{i}") for i in range(S // LOAD)]
+
+        def load_plane(t):
+            nc.sync.dma_start(out=planes[t][:], in_=s_rows[:, t, :])
+
+        def load_codes(i):
+            words = (w1_words, w2_words)[i]
+            nc.sync.dma_start(out=w_codes[i][:].bitcast(I32), in_=words[0].rearrange("p m r -> p (m r)").bitcast(I32))
+
+        def load_scales(i):
+            scales = (w1_scales, w2_scales)[i]
+            for q in range(4):
+                nc.gpsimd.dma_start(
+                    out=w_scales[i][32 * q : 32 * q + 4, :].bitcast(I32),
+                    in_=scales[0, 4 * q : 4 * q + 4, :].bitcast(I32),
+                )
+
+        def load_queries(i):
+            nc.sync.dma_start(out=x_raw[i][:], in_=x_rows[:, :, i * LOAD : (i + 1) * LOAD])
+
+        for plane in w_scales:
+            nc.gpsimd.memset(plane[:].bitcast(I32), 0)
+        load_scales(1)
+        load_scales(0)
+        load_plane(0)
+        nc.sync.dma_start(out=offsets[:], in_=offs)
+        load_plane(1)
+        load_plane(2)
+        load_plane(3)
+        load_queries(0)
+        load_codes(1)
+        load_codes(0)
+        for i in range(1, S // LOAD):
+            load_queries(i)
+
+        acc = [psum.tile([P, n], F32, name=f"acc{b}") for b, (j0, n) in enumerate(BLOCKS)]
+
+        s_packed = keep.tile([P, S, PACK], BF16, align_bytes=64)
+        s_codes = keep.tile([P, S], U32, align_bytes=64)
+        s_scales = keep.tile([P, S], U8, align_bytes=64)
+        x_packed = [keep.tile([P, n, PACK], BF16, name=f"x_packed{b}", align_bytes=64) for b, (j0, n) in enumerate(BLOCKS)]
+        x_codes = [keep.tile([P, n], U32, name=f"x_codes{b}", align_bytes=64) for b, (j0, n) in enumerate(BLOCKS)]
+        x_scales = [keep.tile([P, n], U8, name=f"x_scales{b}", align_bytes=64) for b, (j0, n) in enumerate(BLOCKS)]
+        result = [keep.tile([P, LOAD], F32, name=f"result{i}") for i in range(S // LOAD)]
+
+        def gather(t):
+            nc.vector.tensor_copy(out=s_packed[:, :, t], in_=planes[t][:].indirect(offsets[:]))
+
+        def quantize(packed, codes, scales):
+            nc.vector.quantize_mx(out=codes.bitcast(FP8X4), scales=scales, in_=packed.rearrange("p n t -> p (n t)"))
+
+        def quantize_queries(b):
+            quantize(x_packed[b][:], x_codes[b][:], x_scales[b][:])
+
+        def quantize_memories(j0, j1):
+            quantize(s_packed[:, j0:j1, :], s_codes[:, j0:j1], s_scales[:, j0:j1])
+
+        def memories_times_w2(b):
+            j0, n = BLOCKS[b]
+            cols = slice(j0, j0 + n)
+            nc.tensor.matmul_mx(
+                out=acc[b][:],
+                lhsT=w_codes[1][:].bitcast(FP8X4),
+                lhsT_scale=w_scales[1][:],
+                rhs=s_codes[:, cols].bitcast(FP8X4),
+                rhs_scale=s_scales[:, cols],
+                start=True,
+                stop=False,
+            )
+
+        def queries_times_w1(b):
+            nc.tensor.matmul_mx(
+                out=acc[b][:],
+                lhsT=w_codes[0][:].bitcast(FP8X4),
+                lhsT_scale=w_scales[0][:],
+                rhs=x_codes[b][:].bitcast(FP8X4),
+                rhs_scale=x_scales[b][:],
+                start=False,
+                stop=True,
+            )
+
+        def interleave(copy, b):
+            j0, n = BLOCKS[b]
+            cols = slice(j0 % LOAD, j0 % LOAD + n)
+            copy(
+                out=x_packed[b][:].rearrange("p (c i) t -> p c t i", i=4),
+                in_=x_raw[j0 // LOAD][:, :, cols].rearrange("p t (c i) -> p c t i", i=4),
+            )
+
+        def take_out(copy, b):
+            j0, n = BLOCKS[b]
+            copy(out=result[j0 // LOAD][:, j0 % LOAD : j0 % LOAD + n], in_=acc[b][:])
+
+        def store(i):
+            nc.sync.dma_start(out=out[:, i * LOAD : (i + 1) * LOAD], in_=result[i][:])
+
+        for t in range(PACK):
+            gather(t)
+        for b in range(3):
+            interleave(nc.scalar.copy, b)
+        quantize_queries(0)
+        quantize_memories(0, 512)
+        memories_times_w2(0)
+        queries_times_w1(0)
+        take_out(nc.scalar.copy, 0)
+        store(0)
+        memories_times_w2(1)
+        quantize_memories(512, 1024)
+        for b in range(2, 5):
+            memories_times_w2(b)
+        quantize_queries(1)
+        queries_times_w1(1)
+        quantize_queries(2)
+        queries_times_w1(2)
+        interleave(nc.vector.tensor_copy, 3)
+        interleave(nc.scalar.copy, 4)
+        quantize_queries(4)
+        queries_times_w1(4)
+        quantize_queries(3)
+        queries_times_w1(3)
+        take_out(nc.scalar.copy, 1)
+        store(1)
+        take_out(nc.scalar.copy, 2)
+        store(2)
+        take_out(nc.vector.tensor_copy, 4)
+        take_out(nc.vector.tensor_copy, 3)
+        store(3)

@@ -16,7 +16,10 @@ T = 4096
 S = 1024
 M = 128
 LISTED = 16
-LOAD = 256
+LAST = PACK - 1
+PIECES = ((0, 1536), (1536, 1024), (2560, 1024), (3584, 512))
+HALF = S // 2
+LOADS = ((0, 512), (512, 256), (768, 128), (896, 128))
 BLOCKS = ((0, 256), (256, 256), (512, 256), (768, 128), (896, 128))
 
 FLOPS = 2 * 2 * 512 * M * S
@@ -37,10 +40,14 @@ def tile_picked_recall_none_e_kernel(
         offsets = keep.tile([P, S // LISTED], U16, name="offsets")
         w_codes = [keep.tile([P, M], U32, name=f"w_codes{i}", align_bytes=64) for i in range(2)]
         w_scales = [keep.tile([P, M], U8, name=f"w_scales{i}", align_bytes=64) for i in range(2)]
-        x_raw = [keep.tile([P, PACK, LOAD], F32, name=f"x_raw{i}") for i in range(S // LOAD)]
+        x_raw = [keep.tile([P, PACK, n], F32, name=f"x_raw{i}") for i, (j0, n) in enumerate(LOADS)]
 
         def load_plane(t):
             nc.sync.dma_start(out=planes[t][:], in_=s_rows[:, t, :])
+
+        def load_piece(c):
+            c0, n = PIECES[c]
+            nc.sync.dma_start(out=planes[LAST][:, c0 : c0 + n], in_=s_rows[:, LAST, c0 : c0 + n])
 
         def load_codes(i):
             words = (w1_words, w2_words)[i]
@@ -55,7 +62,8 @@ def tile_picked_recall_none_e_kernel(
                 )
 
         def load_queries(i):
-            nc.sync.dma_start(out=x_raw[i][:], in_=x_rows[:, :, i * LOAD : (i + 1) * LOAD])
+            j0, n = LOADS[i]
+            nc.sync.dma_start(out=x_raw[i][:], in_=x_rows[:, :, j0 : j0 + n])
 
         for plane in w_scales:
             nc.gpsimd.memset(plane[:].bitcast(I32), 0)
@@ -65,25 +73,34 @@ def tile_picked_recall_none_e_kernel(
         nc.sync.dma_start(out=offsets[:], in_=offs)
         load_plane(1)
         load_plane(2)
-        load_plane(3)
+        for c in range(len(PIECES)):
+            load_piece(c)
         load_queries(0)
         load_codes(1)
         load_codes(0)
-        for i in range(1, S // LOAD):
+        for i in range(1, len(LOADS)):
             load_queries(i)
 
         acc = [psum.tile([P, n], F32, name=f"acc{b}") for b, (j0, n) in enumerate(BLOCKS)]
 
         s_packed = keep.tile([P, S, PACK], BF16, align_bytes=64)
+        last_rounded = keep.tile([P, T], BF16)
         s_codes = keep.tile([P, S], U32, align_bytes=64)
         s_scales = keep.tile([P, S], U8, align_bytes=64)
         x_packed = [keep.tile([P, n, PACK], BF16, name=f"x_packed{b}", align_bytes=64) for b, (j0, n) in enumerate(BLOCKS)]
         x_codes = [keep.tile([P, n], U32, name=f"x_codes{b}", align_bytes=64) for b, (j0, n) in enumerate(BLOCKS)]
         x_scales = [keep.tile([P, n], U8, name=f"x_scales{b}", align_bytes=64) for b, (j0, n) in enumerate(BLOCKS)]
-        result = [keep.tile([P, LOAD], F32, name=f"result{i}") for i in range(S // LOAD)]
+        spare = x_raw[2][:].rearrange("p t n -> p (t n)")
+        result = [keep.tile([P, n], F32, name=f"result{b}")[:] for b, (j0, n) in enumerate(BLOCKS)]
+        result[0] = spare[:, :256]
+        result[2] = spare[:, 256:]
 
         def gather(t):
             nc.vector.tensor_copy(out=s_packed[:, :, t], in_=planes[t][:].indirect(offsets[:]))
+
+        def round_piece(copy, c):
+            c0, n = PIECES[c]
+            copy(out=last_rounded[:, c0 : c0 + n], in_=planes[LAST][:, c0 : c0 + n])
 
         def quantize(packed, codes, scales):
             nc.vector.quantize_mx(out=codes.bitcast(FP8X4), scales=scales, in_=packed.rearrange("p n t -> p (n t)"))
@@ -120,47 +137,60 @@ def tile_picked_recall_none_e_kernel(
 
         def interleave(copy, b):
             j0, n = BLOCKS[b]
-            cols = slice(j0 % LOAD, j0 % LOAD + n)
+            i = max(i for i, (first, width) in enumerate(LOADS) if first <= j0)
+            cols = slice(j0 - LOADS[i][0], j0 - LOADS[i][0] + n)
             copy(
                 out=x_packed[b][:].rearrange("p (c i) t -> p c t i", i=4),
-                in_=x_raw[j0 // LOAD][:, :, cols].rearrange("p t (c i) -> p c t i", i=4),
+                in_=x_raw[i][:, :, cols].rearrange("p t (c i) -> p c t i", i=4),
             )
 
         def take_out(copy, b):
+            copy(out=result[b], in_=acc[b][:])
+
+        def store(b):
             j0, n = BLOCKS[b]
-            copy(out=result[j0 // LOAD][:, j0 % LOAD : j0 % LOAD + n], in_=acc[b][:])
+            nc.sync.dma_start(out=out[:, j0 : j0 + n], in_=result[b])
 
-        def store(i):
-            nc.sync.dma_start(out=out[:, i * LOAD : (i + 1) * LOAD], in_=result[i][:])
-
-        for t in range(PACK):
+        for t in range(LAST):
             gather(t)
-        for b in range(3):
-            interleave(nc.scalar.copy, b)
-        quantize_queries(0)
-        quantize_memories(0, 512)
+        round_piece(nc.scalar.copy, 0)
+        round_piece(nc.scalar.copy, 1)
+        round_piece(nc.vector.tensor_copy, 2)
+        round_piece(nc.scalar.copy, 3)
+        nc.vector.tensor_copy(out=s_packed[:, :HALF, LAST], in_=planes[LAST][:].indirect(offsets[:, : HALF // LISTED]))
+        nc.scalar.activation(
+            out=s_packed[:, HALF:, LAST],
+            in_=last_rounded[:].indirect(offsets[:, HALF // LISTED :]),
+            func=mybir.ActivationFunctionType.Copy,
+        )
+        quantize_memories(0, HALF)
         memories_times_w2(0)
-        queries_times_w1(0)
-        take_out(nc.scalar.copy, 0)
-        store(0)
         memories_times_w2(1)
-        quantize_memories(512, 1024)
+        quantize_memories(HALF, S)
         for b in range(2, 5):
             memories_times_w2(b)
+        interleave(nc.scalar.copy, 1)
+        interleave(nc.vector.tensor_copy, 0)
         quantize_queries(1)
         queries_times_w1(1)
-        quantize_queries(2)
-        queries_times_w1(2)
-        interleave(nc.vector.tensor_copy, 3)
-        interleave(nc.scalar.copy, 4)
-        quantize_queries(4)
-        queries_times_w1(4)
-        quantize_queries(3)
-        queries_times_w1(3)
+        quantize_queries(0)
+        queries_times_w1(0)
         take_out(nc.scalar.copy, 1)
         store(1)
+        interleave(nc.vector.tensor_copy, 2)
+        interleave(nc.scalar.copy, 3)
+        quantize_queries(2)
+        queries_times_w1(2)
+        take_out(nc.scalar.copy, 0)
+        store(0)
+        quantize_queries(3)
+        queries_times_w1(3)
+        interleave(nc.vector.tensor_copy, 4)
+        quantize_queries(4)
+        queries_times_w1(4)
         take_out(nc.scalar.copy, 2)
         store(2)
-        take_out(nc.vector.tensor_copy, 4)
-        take_out(nc.vector.tensor_copy, 3)
+        take_out(nc.scalar.copy, 3)
         store(3)
+        take_out(nc.vector.tensor_copy, 4)
+        store(4)

@@ -17,9 +17,9 @@ S = 1024
 M = 128
 LISTED = 16
 LAST = PACK - 1
-PIECES = ((0, 1536), (1536, 1024), (2560, 1024), (3584, 512))
+PIECES = ((0, 2560), (2560, 1024), (3584, 512))
 HALF = S // 2
-LOADS = ((0, 512), (512, 256), (768, 128), (896, 128))
+LOADS = ((0, 256), (256, 256), (512, 256), (768, 128), (896, 128))
 BLOCKS = ((0, 256), (256, 256), (512, 256), (768, 128), (896, 128))
 
 FLOPS = 2 * 2 * 512 * M * S
@@ -40,7 +40,7 @@ def tile_picked_recall_none_e_kernel(
         offsets = keep.tile([P, S // LISTED], U16, name="offsets")
         w_codes = [keep.tile([P, M], U32, name=f"w_codes{i}", align_bytes=64) for i in range(2)]
         w_scales = [keep.tile([P, M], U8, name=f"w_scales{i}", align_bytes=64) for i in range(2)]
-        x_raw = [keep.tile([P, PACK, n], F32, name=f"x_raw{i}") for i, (j0, n) in enumerate(LOADS)]
+        x_raw = [keep.tile([P, PACK, n], F32, name=f"x_raw{i}", tag=f"x_raw{i}", align_bytes=64) for i, (j0, n) in enumerate(LOADS)]
 
         def load_plane(t):
             nc.sync.dma_start(out=planes[t][:], in_=s_rows[:, t, :])
@@ -75,41 +75,45 @@ def tile_picked_recall_none_e_kernel(
         load_plane(2)
         for c in range(len(PIECES)):
             load_piece(c)
-        load_queries(0)
+        for i in range(3):
+            load_queries(i)
         load_codes(1)
         load_codes(0)
-        for i in range(1, len(LOADS)):
+        for i in range(3, len(LOADS)):
             load_queries(i)
 
         acc = [psum.tile([P, n], F32, name=f"acc{b}") for b, (j0, n) in enumerate(BLOCKS)]
 
-        s_packed = keep.tile([P, S, PACK], BF16, align_bytes=64)
+        s_packed = keep.tile([P, S * PACK], BF16, align_bytes=64)
         last_rounded = keep.tile([P, T], BF16)
         s_codes = keep.tile([P, S], U32, align_bytes=64)
         s_scales = keep.tile([P, S], U8, align_bytes=64)
-        x_packed = [keep.tile([P, n, PACK], BF16, name=f"x_packed{b}", align_bytes=64) for b, (j0, n) in enumerate(BLOCKS)]
-        x_codes = [keep.tile([P, n], U32, name=f"x_codes{b}", align_bytes=64) for b, (j0, n) in enumerate(BLOCKS)]
-        x_scales = [keep.tile([P, n], U8, name=f"x_scales{b}", align_bytes=64) for b, (j0, n) in enumerate(BLOCKS)]
-        spare = x_raw[2][:].rearrange("p t n -> p (t n)")
+        x_packed = keep.tile([P, S * PACK], BF16, align_bytes=64)
+        x_codes = keep.tile([P, S], U32, align_bytes=64)
+        x_scales = keep.tile([P, S], U8, align_bytes=64)
         result = [keep.tile([P, n], F32, name=f"result{b}")[:] for b, (j0, n) in enumerate(BLOCKS)]
+        spare = x_raw[3][:].rearrange("p t n -> p (t n)")
         result[0] = spare[:, :256]
-        result[2] = spare[:, 256:]
+        result[1] = spare[:, 256:]
+        result[2] = x_raw[4][:].rearrange("p t n -> p (t n)")[:, :256]
+
+        def slot(j0, j1, t):
+            return s_packed[:, j0 * PACK : j1 * PACK].rearrange("p (n t) -> p n t", t=PACK)[:, :, t]
 
         def gather(t):
-            nc.vector.tensor_copy(out=s_packed[:, :, t], in_=planes[t][:].indirect(offsets[:]))
+            nc.vector.tensor_copy(out=slot(0, S, t), in_=planes[t][:].indirect(offsets[:]))
 
-        def round_piece(copy, c):
-            c0, n = PIECES[c]
-            copy(out=last_rounded[:, c0 : c0 + n], in_=planes[LAST][:, c0 : c0 + n])
+        def round_columns(copy, c0, c1):
+            copy(out=last_rounded[:, c0:c1], in_=planes[LAST][:, c0:c1])
 
         def quantize(packed, codes, scales):
-            nc.vector.quantize_mx(out=codes.bitcast(FP8X4), scales=scales, in_=packed.rearrange("p n t -> p (n t)"))
+            nc.vector.quantize_mx(out=codes.bitcast(FP8X4), scales=scales, in_=packed)
 
-        def quantize_queries(b):
-            quantize(x_packed[b][:], x_codes[b][:], x_scales[b][:])
+        def quantize_queries(j0, j1):
+            quantize(x_packed[:, j0 * PACK : j1 * PACK], x_codes[:, j0:j1], x_scales[:, j0:j1])
 
         def quantize_memories(j0, j1):
-            quantize(s_packed[:, j0:j1, :], s_codes[:, j0:j1], s_scales[:, j0:j1])
+            quantize(s_packed[:, j0 * PACK : j1 * PACK], s_codes[:, j0:j1], s_scales[:, j0:j1])
 
         def memories_times_w2(b):
             j0, n = BLOCKS[b]
@@ -125,23 +129,24 @@ def tile_picked_recall_none_e_kernel(
             )
 
         def queries_times_w1(b):
+            j0, n = BLOCKS[b]
+            cols = slice(j0, j0 + n)
             nc.tensor.matmul_mx(
                 out=acc[b][:],
                 lhsT=w_codes[0][:].bitcast(FP8X4),
                 lhsT_scale=w_scales[0][:],
-                rhs=x_codes[b][:].bitcast(FP8X4),
-                rhs_scale=x_scales[b][:],
+                rhs=x_codes[:, cols].bitcast(FP8X4),
+                rhs_scale=x_scales[:, cols],
                 start=False,
                 stop=True,
             )
 
-        def interleave(copy, b):
-            j0, n = BLOCKS[b]
+        def interleave(copy, j0, j1):
             i = max(i for i, (first, width) in enumerate(LOADS) if first <= j0)
-            cols = slice(j0 - LOADS[i][0], j0 - LOADS[i][0] + n)
+            first = LOADS[i][0]
             copy(
-                out=x_packed[b][:].rearrange("p (c i) t -> p c t i", i=4),
-                in_=x_raw[i][:, :, cols].rearrange("p t (c i) -> p c t i", i=4),
+                out=x_packed[:, j0 * PACK : j1 * PACK].rearrange("p (c i t) -> p c t i", i=4, t=PACK),
+                in_=x_raw[i][:, :, j0 - first : j1 - first].rearrange("p t (c i) -> p c t i", i=4),
             )
 
         def take_out(copy, b):
@@ -153,44 +158,37 @@ def tile_picked_recall_none_e_kernel(
 
         for t in range(LAST):
             gather(t)
-        round_piece(nc.scalar.copy, 0)
-        round_piece(nc.scalar.copy, 1)
-        round_piece(nc.vector.tensor_copy, 2)
-        round_piece(nc.scalar.copy, 3)
-        nc.vector.tensor_copy(out=s_packed[:, :HALF, LAST], in_=planes[LAST][:].indirect(offsets[:, : HALF // LISTED]))
+        round_columns(nc.scalar.copy, 0, 1536)
+        round_columns(nc.vector.tensor_copy, 1536, 2560)
+        round_columns(nc.vector.tensor_copy, 2560, 3584)
+        round_columns(nc.vector.tensor_copy, 3584, T)
+        nc.vector.tensor_copy(out=slot(0, HALF, LAST), in_=planes[LAST][:].indirect(offsets[:, : HALF // LISTED]))
         nc.scalar.activation(
-            out=s_packed[:, HALF:, LAST],
+            out=slot(HALF, S, LAST),
             in_=last_rounded[:].indirect(offsets[:, HALF // LISTED :]),
             func=mybir.ActivationFunctionType.Copy,
         )
+        interleave(nc.vector.tensor_copy, 0, 256)
         quantize_memories(0, HALF)
-        memories_times_w2(0)
-        memories_times_w2(1)
         quantize_memories(HALF, S)
-        for b in range(2, 5):
-            memories_times_w2(b)
-        interleave(nc.scalar.copy, 1)
-        interleave(nc.vector.tensor_copy, 0)
-        quantize_queries(1)
-        queries_times_w1(1)
-        quantize_queries(0)
+        interleave(nc.scalar.copy, 256, 512)
+        quantize_queries(0, 256)
+        interleave(nc.scalar.copy, 512, 768)
+        memories_times_w2(0)
         queries_times_w1(0)
-        take_out(nc.scalar.copy, 1)
-        store(1)
-        interleave(nc.vector.tensor_copy, 2)
-        interleave(nc.scalar.copy, 3)
-        quantize_queries(2)
+        for b in range(1, 5):
+            memories_times_w2(b)
+        quantize_queries(256, 512)
+        queries_times_w1(1)
+        quantize_queries(512, 768)
         queries_times_w1(2)
-        take_out(nc.scalar.copy, 0)
-        store(0)
-        quantize_queries(3)
+        interleave(nc.scalar.copy, 768, 896)
+        interleave(nc.vector.tensor_copy, 896, S)
+        quantize_queries(768, S)
         queries_times_w1(3)
-        interleave(nc.vector.tensor_copy, 4)
-        quantize_queries(4)
         queries_times_w1(4)
-        take_out(nc.scalar.copy, 2)
-        store(2)
-        take_out(nc.scalar.copy, 3)
-        store(3)
+        for b in range(4):
+            take_out(nc.scalar.copy, b)
+            store(b)
         take_out(nc.vector.tensor_copy, 4)
         store(4)

@@ -75,11 +75,11 @@ def tile_picked_recall_none_e_kernel(
         load_plane(2)
         for c in range(len(PIECES)):
             load_piece(c)
-        for i in range(3):
-            load_queries(i)
+        load_queries(0)
         load_codes(1)
+        load_queries(1)
         load_codes(0)
-        for i in range(3, len(LOADS)):
+        for i in range(2, len(LOADS)):
             load_queries(i)
 
         acc = [psum.tile([P, n], F32, name=f"acc{b}") for b, (j0, n) in enumerate(BLOCKS)]
@@ -170,9 +170,9 @@ def tile_picked_recall_none_e_kernel(
         )
         interleave(nc.vector.tensor_copy, 0, 256)
         quantize_memories(0, HALF)
+        quantize_queries(0, 256)
         quantize_memories(HALF, S)
         interleave(nc.scalar.copy, 256, 512)
-        quantize_queries(0, 256)
         interleave(nc.scalar.copy, 512, 768)
         memories_times_w2(0)
         queries_times_w1(0)

@@ -17,10 +17,11 @@ S = 1024
 M = 128
 LISTED = 16
 LAST = PACK - 1
-PIECES = ((0, 2560), (2560, 1024), (3584, 512))
 HALF = S // 2
-LOADS = ((0, 256), (256, 256), (512, 256), (768, 128), (896, 128))
-BLOCKS = ((0, 256), (256, 256), (512, 256), (768, 128), (896, 128))
+
+PIECES = ((0, 2560), (2560, 3584), (3584, T))
+SCALAR_ROUNDS = 1536
+BLOCKS = ((0, 256), (256, 512), (512, 768), (768, 896), (896, S))
 
 FLOPS = 2 * 2 * 512 * M * S
 
@@ -37,158 +38,147 @@ def tile_picked_recall_none_e_kernel(
         x_rows = xT.rearrange("(p t) n -> p t n", t=PACK)
 
         planes = [keep.tile([P, T], F32, name=f"plane{t}") for t in range(PACK)]
-        offsets = keep.tile([P, S // LISTED], U16, name="offsets")
-        w_codes = [keep.tile([P, M], U32, name=f"w_codes{i}", align_bytes=64) for i in range(2)]
-        w_scales = [keep.tile([P, M], U8, name=f"w_scales{i}", align_bytes=64) for i in range(2)]
-        x_raw = [keep.tile([P, PACK, n], F32, name=f"x_raw{i}", tag=f"x_raw{i}", align_bytes=64) for i, (j0, n) in enumerate(LOADS)]
-
-        def load_plane(t):
-            nc.sync.dma_start(out=planes[t][:], in_=s_rows[:, t, :])
-
-        def load_piece(c):
-            c0, n = PIECES[c]
-            nc.sync.dma_start(out=planes[LAST][:, c0 : c0 + n], in_=s_rows[:, LAST, c0 : c0 + n])
-
-        def load_codes(i):
-            words = (w1_words, w2_words)[i]
-            nc.sync.dma_start(out=w_codes[i][:].bitcast(I32), in_=words[0].rearrange("p m r -> p (m r)").bitcast(I32))
-
-        def load_scales(i):
-            scales = (w1_scales, w2_scales)[i]
-            for q in range(4):
-                nc.gpsimd.dma_start(
-                    out=w_scales[i][32 * q : 32 * q + 4, :].bitcast(I32),
-                    in_=scales[0, 4 * q : 4 * q + 4, :].bitcast(I32),
-                )
-
-        def load_queries(i):
-            j0, n = LOADS[i]
-            nc.sync.dma_start(out=x_raw[i][:], in_=x_rows[:, :, j0 : j0 + n])
-
-        for plane in w_scales:
-            nc.gpsimd.memset(plane[:].bitcast(I32), 0)
-        load_scales(1)
-        load_scales(0)
-        load_plane(0)
-        nc.sync.dma_start(out=offsets[:], in_=offs)
-        load_plane(1)
-        load_plane(2)
-        for c in range(len(PIECES)):
-            load_piece(c)
-        load_queries(0)
-        load_codes(1)
-        load_queries(1)
-        load_codes(0)
-        for i in range(2, len(LOADS)):
-            load_queries(i)
-
-        acc = [psum.tile([P, n], F32, name=f"acc{b}") for b, (j0, n) in enumerate(BLOCKS)]
-
+        offsets = keep.tile([P, S // LISTED], U16)
+        w1_codes = keep.tile([P, M], U32, align_bytes=64)
+        w2_codes = keep.tile([P, M], U32, align_bytes=64)
+        w1_bytes = keep.tile([P, M], U8, align_bytes=64)
+        w2_bytes = keep.tile([P, M], U8, align_bytes=64)
+        x_raw = [
+            keep.tile([P, PACK, j1 - j0], F32, name=f"x_raw{b}", align_bytes=64) for b, (j0, j1) in enumerate(BLOCKS)
+        ]
         s_packed = keep.tile([P, S * PACK], BF16, align_bytes=64)
         last_rounded = keep.tile([P, T], BF16)
         s_codes = keep.tile([P, S], U32, align_bytes=64)
-        s_scales = keep.tile([P, S], U8, align_bytes=64)
+        s_bytes = keep.tile([P, S], U8, align_bytes=64)
         x_packed = keep.tile([P, S * PACK], BF16, align_bytes=64)
         x_codes = keep.tile([P, S], U32, align_bytes=64)
-        x_scales = keep.tile([P, S], U8, align_bytes=64)
-        result = [keep.tile([P, n], F32, name=f"result{b}")[:] for b, (j0, n) in enumerate(BLOCKS)]
-        spare = x_raw[3][:].rearrange("p t n -> p (t n)")
-        result[0] = spare[:, :256]
-        result[1] = spare[:, 256:]
-        result[2] = x_raw[4][:].rearrange("p t n -> p (t n)")[:, :256]
+        x_bytes = keep.tile([P, S], U8, align_bytes=64)
+        acc = [psum.tile([P, j1 - j0], F32, name=f"acc{b}") for b, (j0, j1) in enumerate(BLOCKS)]
+
+        raw3 = x_raw[3][:].rearrange("p t n -> p (t n)")
+        raw4 = x_raw[4][:].rearrange("p t n -> p (t n)")
+        tail = [keep.tile([P, j1 - j0], F32, name=f"tail{j0}") for j0, j1 in BLOCKS[3:]]
+        wide = BLOCKS[0][1]
+        result = [raw3[:, :wide], raw3[:, wide:], raw4[:, :wide], tail[0][:], tail[1][:]]
+
+        def load_codes(codes, words):
+            nc.sync.dma_start(out=codes[:].bitcast(I32), in_=words[0].rearrange("p m r -> p (m r)").bitcast(I32))
+
+        def load_scale_bytes(tile, scales):
+            for q in range(4):
+                nc.gpsimd.dma_start(
+                    out=tile[32 * q : 32 * q + 4, :].bitcast(I32),
+                    in_=scales[0, 4 * q : 4 * q + 4, :].bitcast(I32),
+                )
+
+        def load_queries(b):
+            j0, j1 = BLOCKS[b]
+            nc.sync.dma_start(out=x_raw[b][:], in_=x_rows[:, :, j0:j1])
+
+        for tile in (w1_bytes, w2_bytes):
+            nc.gpsimd.memset(tile[:].bitcast(I32), 0)
+        load_scale_bytes(w2_bytes, w2_scales)
+        load_scale_bytes(w1_bytes, w1_scales)
+
+        nc.sync.dma_start(out=planes[0][:], in_=s_rows[:, 0, :])
+        nc.sync.dma_start(out=offsets[:], in_=offs)
+        for t in range(1, LAST):
+            nc.sync.dma_start(out=planes[t][:], in_=s_rows[:, t, :])
+        for c0, c1 in PIECES:
+            nc.sync.dma_start(out=planes[LAST][:, c0:c1], in_=s_rows[:, LAST, c0:c1])
+        load_queries(0)
+        load_codes(w2_codes, w2_words)
+        load_queries(1)
+        load_codes(w1_codes, w1_words)
+        for b in range(2, len(BLOCKS)):
+            load_queries(b)
 
         def slot(j0, j1, t):
             return s_packed[:, j0 * PACK : j1 * PACK].rearrange("p (n t) -> p n t", t=PACK)[:, :, t]
 
-        def gather(t):
-            nc.vector.tensor_copy(out=slot(0, S, t), in_=planes[t][:].indirect(offsets[:]))
+        def entries(j0, j1):
+            return offsets[:, j0 // LISTED : j1 // LISTED]
+
+        def gather(j0, j1, t):
+            nc.vector.tensor_copy(out=slot(j0, j1, t), in_=planes[t][:].indirect(entries(j0, j1)))
 
         def round_columns(copy, c0, c1):
             copy(out=last_rounded[:, c0:c1], in_=planes[LAST][:, c0:c1])
 
-        def quantize(packed, codes, scales):
-            nc.vector.quantize_mx(out=codes.bitcast(FP8X4), scales=scales, in_=packed)
-
-        def quantize_queries(j0, j1):
-            quantize(x_packed[:, j0 * PACK : j1 * PACK], x_codes[:, j0:j1], x_scales[:, j0:j1])
-
-        def quantize_memories(j0, j1):
-            quantize(s_packed[:, j0 * PACK : j1 * PACK], s_codes[:, j0:j1], s_scales[:, j0:j1])
-
-        def memories_times_w2(b):
-            j0, n = BLOCKS[b]
-            cols = slice(j0, j0 + n)
-            nc.tensor.matmul_mx(
-                out=acc[b][:],
-                lhsT=w_codes[1][:].bitcast(FP8X4),
-                lhsT_scale=w_scales[1][:],
-                rhs=s_codes[:, cols].bitcast(FP8X4),
-                rhs_scale=s_scales[:, cols],
-                start=True,
-                stop=False,
-            )
-
-        def queries_times_w1(b):
-            j0, n = BLOCKS[b]
-            cols = slice(j0, j0 + n)
-            nc.tensor.matmul_mx(
-                out=acc[b][:],
-                lhsT=w_codes[0][:].bitcast(FP8X4),
-                lhsT_scale=w_scales[0][:],
-                rhs=x_codes[:, cols].bitcast(FP8X4),
-                rhs_scale=x_scales[:, cols],
-                start=False,
-                stop=True,
-            )
-
-        def interleave(copy, j0, j1):
-            i = max(i for i, (first, width) in enumerate(LOADS) if first <= j0)
-            first = LOADS[i][0]
+        def interleave(copy, b):
+            j0, j1 = BLOCKS[b]
             copy(
                 out=x_packed[:, j0 * PACK : j1 * PACK].rearrange("p (c i t) -> p c t i", i=4, t=PACK),
-                in_=x_raw[i][:, :, j0 - first : j1 - first].rearrange("p t (c i) -> p c t i", i=4),
+                in_=x_raw[b][:].rearrange("p t (c i) -> p c t i", i=4),
             )
 
-        def take_out(copy, b):
-            copy(out=result[b], in_=acc[b][:])
+        def quantize(packed, codes, scale_bytes, j0, j1):
+            nc.vector.quantize_mx(
+                out=codes[:, j0:j1].bitcast(FP8X4),
+                scales=scale_bytes[:, j0:j1],
+                in_=packed[:, j0 * PACK : j1 * PACK],
+            )
 
-        def store(b):
-            j0, n = BLOCKS[b]
-            nc.sync.dma_start(out=out[:, j0 : j0 + n], in_=result[b])
+        def multiply(b, w_codes, w_bytes, codes, scale_bytes, first):
+            j0, j1 = BLOCKS[b]
+            nc.tensor.matmul_mx(
+                out=acc[b][:],
+                lhsT=w_codes[:].bitcast(FP8X4),
+                lhsT_scale=w_bytes[:],
+                rhs=codes[:, j0:j1].bitcast(FP8X4),
+                rhs_scale=scale_bytes[:, j0:j1],
+                start=first,
+                stop=not first,
+            )
+
+        def quantize_memories(j0, j1):
+            quantize(s_packed, s_codes, s_bytes, j0, j1)
+
+        def quantize_queries(j0, j1):
+            quantize(x_packed, x_codes, x_bytes, j0, j1)
+
+        def memories_times_w2(b):
+            multiply(b, w2_codes, w2_bytes, s_codes, s_bytes, True)
+
+        def queries_times_w1(b):
+            multiply(b, w1_codes, w1_bytes, x_codes, x_bytes, False)
+
+        def take_out_and_store(copy, b):
+            j0, j1 = BLOCKS[b]
+            copy(out=result[b], in_=acc[b][:])
+            nc.sync.dma_start(out=out[:, j0:j1], in_=result[b])
 
         for t in range(LAST):
-            gather(t)
-        round_columns(nc.scalar.copy, 0, 1536)
-        round_columns(nc.vector.tensor_copy, 1536, 2560)
-        round_columns(nc.vector.tensor_copy, 2560, 3584)
-        round_columns(nc.vector.tensor_copy, 3584, T)
-        nc.vector.tensor_copy(out=slot(0, HALF, LAST), in_=planes[LAST][:].indirect(offsets[:, : HALF // LISTED]))
+            gather(0, S, t)
+        round_columns(nc.scalar.copy, 0, SCALAR_ROUNDS)
+        round_columns(nc.vector.tensor_copy, SCALAR_ROUNDS, PIECES[0][1])
+        for c0, c1 in PIECES[1:]:
+            round_columns(nc.vector.tensor_copy, c0, c1)
+        gather(0, HALF, LAST)
         nc.scalar.activation(
             out=slot(HALF, S, LAST),
-            in_=last_rounded[:].indirect(offsets[:, HALF // LISTED :]),
+            in_=last_rounded[:].indirect(entries(HALF, S)),
             func=mybir.ActivationFunctionType.Copy,
         )
-        interleave(nc.vector.tensor_copy, 0, 256)
+
+        interleave(nc.vector.tensor_copy, 0)
         quantize_memories(0, HALF)
-        quantize_queries(0, 256)
+        quantize_queries(*BLOCKS[0])
         quantize_memories(HALF, S)
-        interleave(nc.scalar.copy, 256, 512)
-        interleave(nc.scalar.copy, 512, 768)
+        interleave(nc.scalar.copy, 1)
+        interleave(nc.scalar.copy, 2)
         memories_times_w2(0)
         queries_times_w1(0)
-        for b in range(1, 5):
+        for b in range(1, len(BLOCKS)):
             memories_times_w2(b)
-        quantize_queries(256, 512)
-        queries_times_w1(1)
-        quantize_queries(512, 768)
-        queries_times_w1(2)
-        interleave(nc.scalar.copy, 768, 896)
-        interleave(nc.vector.tensor_copy, 896, S)
-        quantize_queries(768, S)
+        for b in (1, 2):
+            quantize_queries(*BLOCKS[b])
+            queries_times_w1(b)
+        interleave(nc.scalar.copy, 3)
+        interleave(nc.vector.tensor_copy, 4)
+        quantize_queries(BLOCKS[3][0], BLOCKS[4][1])
         queries_times_w1(3)
         queries_times_w1(4)
         for b in range(4):
-            take_out(nc.scalar.copy, b)
-            store(b)
-        take_out(nc.vector.tensor_copy, 4)
-        store(4)
+            take_out_and_store(nc.scalar.copy, b)
+        take_out_and_store(nc.vector.tensor_copy, 4)

@@ -22,6 +22,7 @@ HALF = S // 2
 PIECES = ((0, 2560), (2560, 3584), (3584, T))
 SCALAR_ROUNDS = 1536
 BLOCKS = ((0, 256), (256, 512), (512, 768), (768, 896), (896, S))
+LOADS = ((0, 128), (128, 512), (512, 768), (768, 896), (896, S))
 
 FLOPS = 2 * 2 * 512 * M * S
 
@@ -44,7 +45,7 @@ def tile_picked_recall_none_e_kernel(
         w1_bytes = keep.tile([P, M], U8, align_bytes=64)
         w2_bytes = keep.tile([P, M], U8, align_bytes=64)
         x_raw = [
-            keep.tile([P, PACK, j1 - j0], F32, name=f"x_raw{b}", align_bytes=64) for b, (j0, j1) in enumerate(BLOCKS)
+            keep.tile([P, PACK, j1 - j0], F32, name=f"x_raw{b}", align_bytes=64) for b, (j0, j1) in enumerate(LOADS)
         ]
         s_packed = keep.tile([P, S * PACK], BF16, align_bytes=64)
         last_rounded = keep.tile([P, T], BF16)
@@ -55,11 +56,11 @@ def tile_picked_recall_none_e_kernel(
         x_bytes = keep.tile([P, S], U8, align_bytes=64)
         acc = [psum.tile([P, j1 - j0], F32, name=f"acc{b}") for b, (j0, j1) in enumerate(BLOCKS)]
 
+        raw2 = x_raw[2][:].rearrange("p t n -> p (t n)")
         raw3 = x_raw[3][:].rearrange("p t n -> p (t n)")
-        raw4 = x_raw[4][:].rearrange("p t n -> p (t n)")
         tail = [keep.tile([P, j1 - j0], F32, name=f"tail{j0}") for j0, j1 in BLOCKS[3:]]
         wide = BLOCKS[0][1]
-        result = [raw3[:, :wide], raw3[:, wide:], raw4[:, :wide], tail[0][:], tail[1][:]]
+        result = [raw2[:, :wide], raw3[:, :wide], raw3[:, wide:], tail[0][:], tail[1][:]]
 
         def load_codes(codes, words):
             nc.sync.dma_start(out=codes[:].bitcast(I32), in_=words[0].rearrange("p m r -> p (m r)").bitcast(I32))
@@ -72,7 +73,7 @@ def tile_picked_recall_none_e_kernel(
                 )
 
         def load_queries(b):
-            j0, j1 = BLOCKS[b]
+            j0, j1 = LOADS[b]
             nc.sync.dma_start(out=x_raw[b][:], in_=x_rows[:, :, j0:j1])
 
         for tile in (w1_bytes, w2_bytes):
@@ -87,10 +88,10 @@ def tile_picked_recall_none_e_kernel(
         for c0, c1 in PIECES:
             nc.sync.dma_start(out=planes[LAST][:, c0:c1], in_=s_rows[:, LAST, c0:c1])
         load_queries(0)
-        load_codes(w2_codes, w2_words)
         load_queries(1)
+        load_codes(w2_codes, w2_words)
         load_codes(w1_codes, w1_words)
-        for b in range(2, len(BLOCKS)):
+        for b in range(2, len(LOADS)):
             load_queries(b)
 
         def slot(j0, j1, t):
@@ -105,11 +106,11 @@ def tile_picked_recall_none_e_kernel(
         def round_columns(copy, c0, c1):
             copy(out=last_rounded[:, c0:c1], in_=planes[LAST][:, c0:c1])
 
-        def interleave(copy, b):
-            j0, j1 = BLOCKS[b]
+        def interleave(copy, b, j0, j1):
+            first = LOADS[b][0]
             copy(
                 out=x_packed[:, j0 * PACK : j1 * PACK].rearrange("p (c i t) -> p c t i", i=4, t=PACK),
-                in_=x_raw[b][:].rearrange("p t (c i) -> p c t i", i=4),
+                in_=x_raw[b][:, :, j0 - first : j1 - first].rearrange("p t (c i) -> p c t i", i=4),
             )
 
         def quantize(packed, codes, scale_bytes, j0, j1):
@@ -152,8 +153,8 @@ def tile_picked_recall_none_e_kernel(
             gather(0, S, t)
         round_columns(nc.scalar.copy, 0, SCALAR_ROUNDS)
         round_columns(nc.vector.tensor_copy, SCALAR_ROUNDS, PIECES[0][1])
-        for c0, c1 in PIECES[1:]:
-            round_columns(nc.vector.tensor_copy, c0, c1)
+        round_columns(nc.vector.tensor_copy, *PIECES[1])
+        round_columns(nc.scalar.copy, *PIECES[2])
         gather(0, HALF, LAST)
         nc.scalar.activation(
             out=slot(HALF, S, LAST),
@@ -161,24 +162,27 @@ def tile_picked_recall_none_e_kernel(
             func=mybir.ActivationFunctionType.Copy,
         )
 
-        interleave(nc.vector.tensor_copy, 0)
+        interleave(nc.vector.tensor_copy, 0, 0, 128)
         quantize_memories(0, HALF)
-        quantize_queries(*BLOCKS[0])
         quantize_memories(HALF, S)
-        interleave(nc.scalar.copy, 1)
-        interleave(nc.scalar.copy, 2)
-        memories_times_w2(0)
-        queries_times_w1(0)
-        for b in range(1, len(BLOCKS)):
+        for b in range(len(BLOCKS)):
             memories_times_w2(b)
-        for b in (1, 2):
+        interleave(nc.scalar.copy, 1, 128, 256)
+        interleave(nc.scalar.copy, 1, 256, 384)
+        interleave(nc.vector.tensor_copy, 1, 384, 512)
+        for b in (0, 1):
             quantize_queries(*BLOCKS[b])
             queries_times_w1(b)
-        interleave(nc.scalar.copy, 3)
-        interleave(nc.vector.tensor_copy, 4)
-        quantize_queries(BLOCKS[3][0], BLOCKS[4][1])
-        queries_times_w1(3)
-        queries_times_w1(4)
-        for b in range(4):
+        interleave(nc.scalar.copy, 2, 512, 640)
+        interleave(nc.vector.tensor_copy, 2, 640, 768)
+        quantize_queries(*BLOCKS[2])
+        queries_times_w1(2)
+        take_out_and_store(nc.scalar.copy, 0)
+        interleave(nc.scalar.copy, 3, 768, 896)
+        interleave(nc.vector.tensor_copy, 4, 896, S)
+        for b in (3, 4):
+            quantize_queries(*BLOCKS[b])
+            queries_times_w1(b)
+        for b in (1, 2, 3):
             take_out_and_store(nc.scalar.copy, b)
         take_out_and_store(nc.vector.tensor_copy, 4)

@@ -38,14 +38,14 @@ def tile_picked_recall_none_e_kernel(
         s_rows = sT.rearrange("(p t) n -> p t n", t=PACK)
         x_rows = xT.rearrange("(p t) n -> p t n", t=PACK)
 
-        planes = [keep.tile([P, T], F32, name=f"plane{t}") for t in range(PACK)]
+        planes = [keep.tile([P, T], F32, name=f"plane{t}", align_bytes=256) for t in range(PACK)]
         offsets = keep.tile([P, S // LISTED], U16)
-        w1_codes = keep.tile([P, M], U32, align_bytes=64)
-        w2_codes = keep.tile([P, M], U32, align_bytes=64)
+        w1_codes = keep.tile([P, M], U32, align_bytes=256)
+        w2_codes = keep.tile([P, M], U32, align_bytes=256)
         w1_bytes = keep.tile([P, M], U8, align_bytes=64)
         w2_bytes = keep.tile([P, M], U8, align_bytes=64)
         x_raw = [
-            keep.tile([P, PACK, j1 - j0], F32, name=f"x_raw{b}", align_bytes=64) for b, (j0, j1) in enumerate(LOADS)
+            keep.tile([P, PACK, j1 - j0], F32, name=f"x_raw{b}", align_bytes=256) for b, (j0, j1) in enumerate(LOADS)
         ]
         s_packed = keep.tile([P, S * PACK], BF16, align_bytes=64)
         last_rounded = keep.tile([P, T], BF16)
@@ -58,7 +58,7 @@ def tile_picked_recall_none_e_kernel(
 
         raw2 = x_raw[2][:].rearrange("p t n -> p (t n)")
         raw3 = x_raw[3][:].rearrange("p t n -> p (t n)")
-        tail = [keep.tile([P, j1 - j0], F32, name=f"tail{j0}") for j0, j1 in BLOCKS[3:]]
+        tail = [keep.tile([P, j1 - j0], F32, name=f"tail{j0}", align_bytes=256) for j0, j1 in BLOCKS[3:]]
         wide = BLOCKS[0][1]
         result = [raw2[:, :wide], raw3[:, :wide], raw3[:, wide:], tail[0][:], tail[1][:]]
 

@@ -21,6 +21,7 @@ HALF = S // 2
 
 PIECES = ((0, 2560), (2560, 3584), (3584, T))
 SCALAR_ROUNDS = 1536
+VECTOR_ROUNDS = 1536
 BLOCKS = ((0, 256), (256, 512), (512, 768), (768, 896), (896, S))
 LOADS = ((0, 128), (128, 512), (512, 768), (768, 896), (896, S))
 
@@ -38,7 +39,10 @@ def tile_picked_recall_none_e_kernel(
         s_rows = sT.rearrange("(p t) n -> p t n", t=PACK)
         x_rows = xT.rearrange("(p t) n -> p t n", t=PACK)
 
-        planes = [keep.tile([P, T], F32, name=f"plane{t}", align_bytes=256) for t in range(PACK)]
+        middle = keep.tile([P, 2 * T], F32, align_bytes=256)
+        first = keep.tile([P, T], F32, align_bytes=256)
+        last = keep.tile([P, T], F32, align_bytes=256)
+        planes = [first[:], middle[:, :T], middle[:, T:], last[:]]
         offsets = keep.tile([P, S // LISTED], U16)
         w1_codes = keep.tile([P, M], U32, align_bytes=256)
         w2_codes = keep.tile([P, M], U32, align_bytes=256)
@@ -48,7 +52,7 @@ def tile_picked_recall_none_e_kernel(
             keep.tile([P, PACK, j1 - j0], F32, name=f"x_raw{b}", align_bytes=256) for b, (j0, j1) in enumerate(LOADS)
         ]
         s_packed = keep.tile([P, S * PACK], BF16, align_bytes=64)
-        last_rounded = keep.tile([P, T], BF16)
+        rounded = keep.tile([P, T], BF16)
         s_codes = keep.tile([P, S], U32, align_bytes=64)
         s_bytes = keep.tile([P, S], U8, align_bytes=64)
         x_packed = keep.tile([P, S * PACK], BF16, align_bytes=64)
@@ -81,10 +85,9 @@ def tile_picked_recall_none_e_kernel(
         load_scale_bytes(w2_bytes, w2_scales)
         load_scale_bytes(w1_bytes, w1_scales)
 
-        nc.sync.dma_start(out=planes[0][:], in_=s_rows[:, 0, :])
+        nc.sync.dma_start(out=middle[:], in_=s_rows[:, 1:LAST, :].rearrange("p t n -> p (t n)"))
         nc.sync.dma_start(out=offsets[:], in_=offs)
-        for t in range(1, LAST):
-            nc.sync.dma_start(out=planes[t][:], in_=s_rows[:, t, :])
+        nc.sync.dma_start(out=first[:], in_=s_rows[:, 0, :])
         for c0, c1 in PIECES:
             nc.sync.dma_start(out=planes[LAST][:, c0:c1], in_=s_rows[:, LAST, c0:c1])
         load_queries(0)
@@ -101,10 +104,17 @@ def tile_picked_recall_none_e_kernel(
             return offsets[:, j0 // LISTED : j1 // LISTED]
 
         def gather(j0, j1, t):
-            nc.vector.tensor_copy(out=slot(j0, j1, t), in_=planes[t][:].indirect(entries(j0, j1)))
+            nc.vector.tensor_copy(out=slot(j0, j1, t), in_=planes[t].indirect(entries(j0, j1)))
 
-        def round_columns(copy, c0, c1):
-            copy(out=last_rounded[:, c0:c1], in_=planes[LAST][:, c0:c1])
+        def round_columns(copy, t, c0, c1):
+            copy(out=rounded[:, c0:c1], in_=planes[t][:, c0:c1])
+
+        def gather_rounded(j0, j1, t):
+            nc.scalar.activation(
+                out=slot(j0, j1, t),
+                in_=rounded[:].indirect(entries(j0, j1)),
+                func=mybir.ActivationFunctionType.Copy,
+            )
 
         def interleave(copy, b, j0, j1):
             first = LOADS[b][0]
@@ -149,18 +159,17 @@ def tile_picked_recall_none_e_kernel(
             copy(out=result[b], in_=acc[b][:])
             nc.sync.dma_start(out=out[:, j0:j1], in_=result[b])
 
-        for t in range(LAST):
-            gather(0, S, t)
-        round_columns(nc.scalar.copy, 0, SCALAR_ROUNDS)
-        round_columns(nc.vector.tensor_copy, SCALAR_ROUNDS, PIECES[0][1])
-        round_columns(nc.vector.tensor_copy, *PIECES[1])
-        round_columns(nc.scalar.copy, *PIECES[2])
+        round_columns(nc.vector.tensor_copy, 2, 0, VECTOR_ROUNDS)
+        round_columns(nc.scalar.copy, 2, VECTOR_ROUNDS, T)
+        gather(0, S, 1)
+        gather_rounded(0, S, 2)
+        gather(0, S, 0)
+        round_columns(nc.scalar.copy, LAST, 0, SCALAR_ROUNDS)
+        round_columns(nc.vector.tensor_copy, LAST, SCALAR_ROUNDS, PIECES[0][1])
+        round_columns(nc.vector.tensor_copy, LAST, *PIECES[1])
+        round_columns(nc.scalar.copy, LAST, *PIECES[2])
         gather(0, HALF, LAST)
-        nc.scalar.activation(
-            out=slot(HALF, S, LAST),
-            in_=last_rounded[:].indirect(entries(HALF, S)),
-            func=mybir.ActivationFunctionType.Copy,
-        )
+        gather_rounded(HALF, S, LAST)
 
         interleave(nc.vector.tensor_copy, 0, 0, 128)
         quantize_memories(0, HALF)

@@ -19,11 +19,13 @@ LISTED = 16
 LAST = PACK - 1
 HALF = S // 2
 
-PIECES = ((0, 2560), (2560, 3584), (3584, T))
-SCALAR_ROUNDS = 1536
+PIECES = ((0, 2560), (2560, 3776), (3776, T))
+SCALAR_ROUNDS = (1280, 384, 320)
 VECTOR_ROUNDS = 1536
 BLOCKS = ((0, 256), (256, 512), (512, 768), (768, 896), (896, S))
 LOADS = ((0, 128), (128, 512), (512, 768), (768, 896), (896, S))
+
+X_TILES = ((0, 128), (128, 768), (768, 896), (896, S))
 
 FLOPS = 2 * 2 * 512 * M * S
 
@@ -48,8 +50,8 @@ def tile_picked_recall_none_e_kernel(
         w2_codes = keep.tile([P, M], U32, align_bytes=256)
         w1_bytes = keep.tile([P, M], U8, align_bytes=64)
         w2_bytes = keep.tile([P, M], U8, align_bytes=64)
-        x_raw = [
-            keep.tile([P, PACK, j1 - j0], F32, name=f"x_raw{b}", align_bytes=256) for b, (j0, j1) in enumerate(LOADS)
+        x_tiles = [
+            keep.tile([P, PACK, j1 - j0], F32, name=f"x_raw{j0}", align_bytes=256) for j0, j1 in X_TILES
         ]
         s_packed = keep.tile([P, S * PACK], BF16, align_bytes=64)
         rounded = keep.tile([P, T], BF16)
@@ -60,11 +62,15 @@ def tile_picked_recall_none_e_kernel(
         x_bytes = keep.tile([P, S], U8, align_bytes=64)
         acc = [psum.tile([P, j1 - j0], F32, name=f"acc{b}") for b, (j0, j1) in enumerate(BLOCKS)]
 
-        raw2 = x_raw[2][:].rearrange("p t n -> p (t n)")
-        raw3 = x_raw[3][:].rearrange("p t n -> p (t n)")
+        raw1 = x_tiles[1][:].rearrange("p t n -> p (t n)")
+        raw2 = x_tiles[2][:].rearrange("p t n -> p (t n)")
         tail = [keep.tile([P, j1 - j0], F32, name=f"tail{j0}", align_bytes=256) for j0, j1 in BLOCKS[3:]]
         wide = BLOCKS[0][1]
-        result = [raw2[:, :wide], raw3[:, :wide], raw3[:, wide:], tail[0][:], tail[1][:]]
+        result = [raw1[:, wide : 2 * wide], raw2[:, :wide], raw2[:, wide:]] + [tile[:] for tile in tail]
+
+        def raw_queries(j0, j1):
+            (first,) = [i for i, (lo, hi) in enumerate(X_TILES) if lo <= j0 and j1 <= hi]
+            return x_tiles[first][:, :, j0 - X_TILES[first][0] : j1 - X_TILES[first][0]]
 
         def load_codes(codes, words):
             nc.sync.dma_start(out=codes[:].bitcast(I32), in_=words[0].rearrange("p m r -> p (m r)").bitcast(I32))
@@ -78,7 +84,7 @@ def tile_picked_recall_none_e_kernel(
 
         def load_queries(b):
             j0, j1 = LOADS[b]
-            nc.sync.dma_start(out=x_raw[b][:], in_=x_rows[:, :, j0:j1])
+            nc.sync.dma_start(out=raw_queries(j0, j1), in_=x_rows[:, :, j0:j1])
 
         for tile in (w1_bytes, w2_bytes):
             nc.gpsimd.memset(tile[:].bitcast(I32), 0)
@@ -116,11 +122,10 @@ def tile_picked_recall_none_e_kernel(
                 func=mybir.ActivationFunctionType.Copy,
             )
 
-        def interleave(copy, b, j0, j1):
-            first = LOADS[b][0]
+        def interleave(copy, j0, j1):
             copy(
                 out=x_packed[:, j0 * PACK : j1 * PACK].rearrange("p (c i t) -> p c t i", i=4, t=PACK),
-                in_=x_raw[b][:, :, j0 - first : j1 - first].rearrange("p t (c i) -> p c t i", i=4),
+                in_=raw_queries(j0, j1).rearrange("p t (c i) -> p c t i", i=4),
             )
 
         def quantize(packed, codes, scale_bytes, j0, j1):
@@ -164,31 +169,30 @@ def tile_picked_recall_none_e_kernel(
         gather(0, S, 1)
         gather_rounded(0, S, 2)
         gather(0, S, 0)
-        round_columns(nc.scalar.copy, LAST, 0, SCALAR_ROUNDS)
-        round_columns(nc.vector.tensor_copy, LAST, SCALAR_ROUNDS, PIECES[0][1])
-        round_columns(nc.vector.tensor_copy, LAST, *PIECES[1])
-        round_columns(nc.scalar.copy, LAST, *PIECES[2])
+        for (c0, c1), share in zip(PIECES, SCALAR_ROUNDS):
+            round_columns(nc.scalar.copy, LAST, c0, c0 + share)
+            if c0 + share < c1:
+                round_columns(nc.vector.tensor_copy, LAST, c0 + share, c1)
         gather(0, HALF, LAST)
         gather_rounded(HALF, S, LAST)
 
-        interleave(nc.vector.tensor_copy, 0, 0, 128)
+        interleave(nc.vector.tensor_copy, 0, 128)
         quantize_memories(0, HALF)
         quantize_memories(HALF, S)
         for b in range(len(BLOCKS)):
             memories_times_w2(b)
-        interleave(nc.scalar.copy, 1, 128, 256)
-        interleave(nc.scalar.copy, 1, 256, 384)
-        interleave(nc.vector.tensor_copy, 1, 384, 512)
-        for b in (0, 1):
+        interleave(nc.scalar.copy, 128, 256)
+        interleave(nc.scalar.copy, 256, 448)
+        quantize_queries(*BLOCKS[0])
+        queries_times_w1(0)
+        interleave(nc.vector.tensor_copy, 528, 768)
+        interleave(nc.scalar.copy, 448, 528)
+        for b in (1, 2):
             quantize_queries(*BLOCKS[b])
             queries_times_w1(b)
-        interleave(nc.scalar.copy, 2, 512, 640)
-        interleave(nc.vector.tensor_copy, 2, 640, 768)
-        quantize_queries(*BLOCKS[2])
-        queries_times_w1(2)
         take_out_and_store(nc.scalar.copy, 0)
-        interleave(nc.scalar.copy, 3, 768, 896)
-        interleave(nc.vector.tensor_copy, 4, 896, S)
+        interleave(nc.scalar.copy, 768, 896)
+        interleave(nc.vector.tensor_copy, 896, S)
         for b in (3, 4):
             quantize_queries(*BLOCKS[b])
             queries_times_w1(b)

@@ -62,11 +62,11 @@ def tile_picked_recall_none_e_kernel(
         x_bytes = keep.tile([P, S], U8, align_bytes=64)
         acc = [psum.tile([P, j1 - j0], F32, name=f"acc{b}") for b, (j0, j1) in enumerate(BLOCKS)]
 
-        raw1 = x_tiles[1][:].rearrange("p t n -> p (t n)")
         raw2 = x_tiles[2][:].rearrange("p t n -> p (t n)")
+        raw3 = x_tiles[3][:].rearrange("p t n -> p (t n)")
         tail = [keep.tile([P, j1 - j0], F32, name=f"tail{j0}", align_bytes=256) for j0, j1 in BLOCKS[3:]]
         wide = BLOCKS[0][1]
-        result = [raw1[:, wide : 2 * wide], raw2[:, :wide], raw2[:, wide:]] + [tile[:] for tile in tail]
+        result = [raw2[:, :wide], raw2[:, wide:], raw3[:, :wide]] + [tile[:] for tile in tail]
 
         def raw_queries(j0, j1):
             (first,) = [i for i, (lo, hi) in enumerate(X_TILES) if lo <= j0 and j1 <= hi]
@@ -99,8 +99,9 @@ def tile_picked_recall_none_e_kernel(
         load_queries(0)
         load_queries(1)
         load_codes(w2_codes, w2_words)
+        load_queries(2)
         load_codes(w1_codes, w1_words)
-        for b in range(2, len(LOADS)):
+        for b in range(3, len(LOADS)):
             load_queries(b)
 
         def slot(j0, j1, t):
@@ -190,12 +191,11 @@ def tile_picked_recall_none_e_kernel(
         for b in (1, 2):
             quantize_queries(*BLOCKS[b])
             queries_times_w1(b)
-        take_out_and_store(nc.scalar.copy, 0)
         interleave(nc.scalar.copy, 768, 896)
         interleave(nc.vector.tensor_copy, 896, S)
         for b in (3, 4):
             quantize_queries(*BLOCKS[b])
             queries_times_w1(b)
-        for b in (1, 2, 3):
+        for b in range(4):
             take_out_and_store(nc.scalar.copy, b)
         take_out_and_store(nc.vector.tensor_copy, 4)

@@ -75,9 +75,9 @@ def tile_picked_recall_none_e_kernel(
         def load_codes(codes, words):
             nc.sync.dma_start(out=codes[:].bitcast(I32), in_=words[0].rearrange("p m r -> p (m r)").bitcast(I32))
 
-        def load_scale_bytes(tile, scales):
-            for q in range(4):
-                nc.gpsimd.dma_start(
+        def load_scale_bytes(tile, scales, queues):
+            for q, queue in enumerate(queues):
+                queue.dma_start(
                     out=tile[32 * q : 32 * q + 4, :].bitcast(I32),
                     in_=scales[0, 4 * q : 4 * q + 4, :].bitcast(I32),
                 )
@@ -88,8 +88,7 @@ def tile_picked_recall_none_e_kernel(
 
         for tile in (w1_bytes, w2_bytes):
             nc.gpsimd.memset(tile[:].bitcast(I32), 0)
-        load_scale_bytes(w2_bytes, w2_scales)
-        load_scale_bytes(w1_bytes, w1_scales)
+        load_scale_bytes(w2_bytes, w2_scales, [nc.gpsimd] * 4)
 
         nc.sync.dma_start(out=middle[:], in_=s_rows[:, 1:LAST, :].rearrange("p t n -> p (t n)"))
         nc.sync.dma_start(out=offsets[:], in_=offs)
@@ -99,6 +98,7 @@ def tile_picked_recall_none_e_kernel(
         load_queries(0)
         load_queries(1)
         load_codes(w2_codes, w2_words)
+        load_scale_bytes(w1_bytes, w1_scales, [nc.gpsimd] + [nc.sync] * 3)
         load_queries(2)
         load_codes(w1_codes, w1_words)
         for b in range(3, len(LOADS)):

@@ -19,8 +19,8 @@ LISTED = 16
 LAST = PACK - 1
 HALF = S // 2
 
-PIECES = ((0, 2560), (2560, 3776), (3776, T))
-SCALAR_ROUNDS = (1280, 384, 320)
+PIECES = ((0, 2688), (2688, 3776), (3776, T))
+SCALAR_ROUNDS = (1088, 320, 320)
 VECTOR_ROUNDS = 1536
 BLOCKS = ((0, 256), (256, 512), (512, 768), (768, 896), (896, S))
 LOADS = ((0, 128), (128, 512), (512, 768), (768, 896), (896, S))
@@ -75,8 +75,8 @@ def tile_picked_recall_none_e_kernel(
         def load_codes(codes, words):
             nc.sync.dma_start(out=codes[:].bitcast(I32), in_=words[0].rearrange("p m r -> p (m r)").bitcast(I32))
 
-        def load_scale_bytes(tile, scales, queues):
-            for q, queue in enumerate(queues):
+        def load_scale_rows(queue, tile, scales, quadrants):
+            for q in quadrants:
                 queue.dma_start(
                     out=tile[32 * q : 32 * q + 4, :].bitcast(I32),
                     in_=scales[0, 4 * q : 4 * q + 4, :].bitcast(I32),
@@ -88,19 +88,20 @@ def tile_picked_recall_none_e_kernel(
 
         for tile in (w1_bytes, w2_bytes):
             nc.gpsimd.memset(tile[:].bitcast(I32), 0)
-        load_scale_bytes(w2_bytes, w2_scales, [nc.gpsimd] * 4)
+        load_scale_rows(nc.gpsimd, w2_bytes, w2_scales, (0, 1))
 
         nc.sync.dma_start(out=middle[:], in_=s_rows[:, 1:LAST, :].rearrange("p t n -> p (t n)"))
         nc.sync.dma_start(out=offsets[:], in_=offs)
         nc.sync.dma_start(out=first[:], in_=s_rows[:, 0, :])
+        load_scale_rows(nc.sync, w2_bytes, w2_scales, (2, 3))
         for c0, c1 in PIECES:
             nc.sync.dma_start(out=planes[LAST][:, c0:c1], in_=s_rows[:, LAST, c0:c1])
         load_queries(0)
         load_queries(1)
         load_codes(w2_codes, w2_words)
-        load_scale_bytes(w1_bytes, w1_scales, [nc.gpsimd] + [nc.sync] * 3)
         load_queries(2)
         load_codes(w1_codes, w1_words)
+        load_scale_rows(nc.sync, w1_bytes, w1_scales, range(4))
         for b in range(3, len(LOADS)):
             load_queries(b)
 

@@ -21,11 +21,11 @@ HALF = S // 2
 
 PIECES = ((0, 2688), (2688, 3776), (3776, T))
 SCALAR_ROUNDS = (1088, 320, 320)
-VECTOR_ROUNDS = 1536
+VECTOR_ROUNDS = 1024
 BLOCKS = ((0, 256), (256, 512), (512, 768), (768, 896), (896, S))
-LOADS = ((0, 128), (128, 512), (512, 768), (768, 896), (896, S))
+LOADS = ((0, 512), (512, 768), (768, 896), (896, S))
 
-X_TILES = ((0, 128), (128, 768), (768, 896), (896, S))
+X_TILES = ((0, 768), (768, 896), (896, S))
 
 FLOPS = 2 * 2 * 512 * M * S
 
@@ -62,8 +62,8 @@ def tile_picked_recall_none_e_kernel(
         x_bytes = keep.tile([P, S], U8, align_bytes=64)
         acc = [psum.tile([P, j1 - j0], F32, name=f"acc{b}") for b, (j0, j1) in enumerate(BLOCKS)]
 
-        raw2 = x_tiles[2][:].rearrange("p t n -> p (t n)")
-        raw3 = x_tiles[3][:].rearrange("p t n -> p (t n)")
+        raw2 = x_tiles[1][:].rearrange("p t n -> p (t n)")
+        raw3 = x_tiles[2][:].rearrange("p t n -> p (t n)")
         tail = [keep.tile([P, j1 - j0], F32, name=f"tail{j0}", align_bytes=256) for j0, j1 in BLOCKS[3:]]
         wide = BLOCKS[0][1]
         result = [raw2[:, :wide], raw2[:, wide:], raw3[:, :wide]] + [tile[:] for tile in tail]
@@ -88,21 +88,20 @@ def tile_picked_recall_none_e_kernel(
 
         for tile in (w1_bytes, w2_bytes):
             nc.gpsimd.memset(tile[:].bitcast(I32), 0)
-        load_scale_rows(nc.gpsimd, w2_bytes, w2_scales, (0, 1))
+        load_scale_rows(nc.gpsimd, w2_bytes, w2_scales, (0,))
 
         nc.sync.dma_start(out=middle[:], in_=s_rows[:, 1:LAST, :].rearrange("p t n -> p (t n)"))
         nc.sync.dma_start(out=offsets[:], in_=offs)
         nc.sync.dma_start(out=first[:], in_=s_rows[:, 0, :])
-        load_scale_rows(nc.sync, w2_bytes, w2_scales, (2, 3))
+        load_scale_rows(nc.sync, w2_bytes, w2_scales, (1, 2, 3))
         for c0, c1 in PIECES:
             nc.sync.dma_start(out=planes[LAST][:, c0:c1], in_=s_rows[:, LAST, c0:c1])
         load_queries(0)
-        load_queries(1)
         load_codes(w2_codes, w2_words)
-        load_queries(2)
+        load_queries(1)
         load_codes(w1_codes, w1_words)
         load_scale_rows(nc.sync, w1_bytes, w1_scales, range(4))
-        for b in range(3, len(LOADS)):
+        for b in range(2, len(LOADS)):
             load_queries(b)
 
         def slot(j0, j1, t):
@@ -178,18 +177,16 @@ def tile_picked_recall_none_e_kernel(
         gather(0, HALF, LAST)
         gather_rounded(HALF, S, LAST)
 
-        interleave(nc.vector.tensor_copy, 0, 128)
         quantize_memories(0, HALF)
         quantize_memories(HALF, S)
         for b in range(len(BLOCKS)):
             memories_times_w2(b)
-        interleave(nc.scalar.copy, 128, 256)
-        interleave(nc.scalar.copy, 256, 448)
-        quantize_queries(*BLOCKS[0])
-        queries_times_w1(0)
-        interleave(nc.vector.tensor_copy, 528, 768)
-        interleave(nc.scalar.copy, 448, 528)
-        for b in (1, 2):
+        interleave(nc.scalar.copy, 0, 256)
+        interleave(nc.vector.tensor_copy, 256, 384)
+        interleave(nc.vector.tensor_copy, 576, 768)
+        interleave(nc.scalar.copy, 384, 528)
+        interleave(nc.scalar.copy, 528, 576)
+        for b in (0, 1, 2):
             quantize_queries(*BLOCKS[b])
             queries_times_w1(b)
         interleave(nc.scalar.copy, 768, 896)

@@ -64,9 +64,9 @@ def tile_picked_recall_none_e_kernel(
 
         raw2 = x_tiles[1][:].rearrange("p t n -> p (t n)")
         raw3 = x_tiles[2][:].rearrange("p t n -> p (t n)")
-        tail = [keep.tile([P, j1 - j0], F32, name=f"tail{j0}", align_bytes=256) for j0, j1 in BLOCKS[3:]]
         wide = BLOCKS[0][1]
-        result = [raw2[:, :wide], raw2[:, wide:], raw3[:, :wide]] + [tile[:] for tile in tail]
+        tail = keep.tile([P, wide], F32, align_bytes=256)
+        result = [raw2[:, :wide], raw2[:, wide:], raw3[:, :wide], tail[:, : wide // 2], tail[:, wide // 2 :]]
 
         def raw_queries(j0, j1):
             (first,) = [i for i, (lo, hi) in enumerate(X_TILES) if lo <= j0 and j1 <= hi]
@@ -88,12 +88,11 @@ def tile_picked_recall_none_e_kernel(
 
         for tile in (w1_bytes, w2_bytes):
             nc.gpsimd.memset(tile[:].bitcast(I32), 0)
-        load_scale_rows(nc.gpsimd, w2_bytes, w2_scales, (0,))
 
         nc.sync.dma_start(out=middle[:], in_=s_rows[:, 1:LAST, :].rearrange("p t n -> p (t n)"))
         nc.sync.dma_start(out=offsets[:], in_=offs)
         nc.sync.dma_start(out=first[:], in_=s_rows[:, 0, :])
-        load_scale_rows(nc.sync, w2_bytes, w2_scales, (1, 2, 3))
+        load_scale_rows(nc.sync, w2_bytes, w2_scales, range(4))
         for c0, c1 in PIECES:
             nc.sync.dma_start(out=planes[LAST][:, c0:c1], in_=s_rows[:, LAST, c0:c1])
         load_queries(0)
@@ -194,6 +193,8 @@ def tile_picked_recall_none_e_kernel(
         for b in (3, 4):
             quantize_queries(*BLOCKS[b])
             queries_times_w1(b)
-        for b in range(4):
+        for b in range(3):
             take_out_and_store(nc.scalar.copy, b)
-        take_out_and_store(nc.vector.tensor_copy, 4)
+        for b in (3, 4):
+            nc.vector.tensor_copy(out=result[b], in_=acc[b][:])
+        nc.sync.dma_start(out=out[:, BLOCKS[3][0] :], in_=tail[:])

@@ -19,9 +19,9 @@ LISTED = 16
 LAST = PACK - 1
 HALF = S // 2
 
-PIECES = ((0, 2688), (2688, 3776), (3776, T))
-SCALAR_ROUNDS = (1088, 320, 320)
-VECTOR_ROUNDS = 1024
+PIECES = ((0, 2432), (2432, 3776), (3776, T))
+SCALAR_ROUNDS = (1408, 256, 320)
+VECTOR_ROUNDS = 1536
 BLOCKS = ((0, 256), (256, 512), (512, 768), (768, 896), (896, S))
 LOADS = ((0, 512), (512, 768), (768, 896), (896, S))
 

@@ -23,9 +23,9 @@ PIECES = ((0, 2432), (2432, 3776), (3776, T))
 SCALAR_ROUNDS = (1408, 256, 320)
 VECTOR_ROUNDS = 1536
 BLOCKS = ((0, 256), (256, 512), (512, 768), (768, 896), (896, S))
-LOADS = ((0, 512), (512, 768), (768, 896), (896, S))
+LOADS = ((0, 384), (384, 768), (768, 896), (896, S))
 
-X_TILES = ((0, 768), (768, 896), (896, S))
+X_TILES = LOADS
 
 FLOPS = 2 * 2 * 512 * M * S
 
@@ -48,8 +48,6 @@ def tile_picked_recall_none_e_kernel(
         offsets = keep.tile([P, S // LISTED], U16)
         w1_codes = keep.tile([P, M], U32, align_bytes=256)
         w2_codes = keep.tile([P, M], U32, align_bytes=256)
-        w1_bytes = keep.tile([P, M], U8, align_bytes=64)
-        w2_bytes = keep.tile([P, M], U8, align_bytes=64)
         x_tiles = [
             keep.tile([P, PACK, j1 - j0], F32, name=f"x_raw{j0}", align_bytes=256) for j0, j1 in X_TILES
         ]
@@ -57,16 +55,19 @@ def tile_picked_recall_none_e_kernel(
         rounded = keep.tile([P, T], BF16)
         s_codes = keep.tile([P, S], U32, align_bytes=64)
         s_bytes = keep.tile([P, S], U8, align_bytes=64)
-        x_packed = keep.tile([P, S * PACK], BF16, align_bytes=64)
+        x_packed = keep.tile([P, S * PACK], BF16, align_bytes=256)
         x_codes = keep.tile([P, S], U32, align_bytes=64)
         x_bytes = keep.tile([P, S], U8, align_bytes=64)
         acc = [psum.tile([P, j1 - j0], F32, name=f"acc{b}") for b, (j0, j1) in enumerate(BLOCKS)]
 
-        raw2 = x_tiles[1][:].rearrange("p t n -> p (t n)")
-        raw3 = x_tiles[2][:].rearrange("p t n -> p (t n)")
+        raw2 = x_tiles[2][:].rearrange("p t n -> p (t n)")
         wide = BLOCKS[0][1]
         tail = keep.tile([P, wide], F32, align_bytes=256)
+        raw3 = x_tiles[3][:].rearrange("p t n -> p (t n)")
         result = [raw2[:, :wide], raw2[:, wide:], raw3[:, :wide], tail[:, : wide // 2], tail[:, wide // 2 :]]
+
+        w1_bytes = s_bytes[:, HALF : HALF + M]
+        w2_bytes = s_bytes[:, :M]
 
         def raw_queries(j0, j1):
             (first,) = [i for i, (lo, hi) in enumerate(X_TILES) if lo <= j0 and j1 <= hi]
@@ -78,7 +79,7 @@ def tile_picked_recall_none_e_kernel(
         def load_scale_rows(queue, tile, scales, quadrants):
             for q in quadrants:
                 queue.dma_start(
-                    out=tile[32 * q : 32 * q + 4, :].bitcast(I32),
+                    out=tile[32 * q + 4 : 32 * q + 8, :].bitcast(I32),
                     in_=scales[0, 4 * q : 4 * q + 4, :].bitcast(I32),
                 )
 
@@ -86,20 +87,25 @@ def tile_picked_recall_none_e_kernel(
             j0, j1 = LOADS[b]
             nc.sync.dma_start(out=raw_queries(j0, j1), in_=x_rows[:, :, j0:j1])
 
-        for tile in (w1_bytes, w2_bytes):
-            nc.gpsimd.memset(tile[:].bitcast(I32), 0)
+        def load_piece(i):
+            c0, c1 = PIECES[i]
+            nc.sync.dma_start(out=planes[LAST][:, c0:c1], in_=s_rows[:, LAST, c0:c1])
 
         nc.sync.dma_start(out=middle[:], in_=s_rows[:, 1:LAST, :].rearrange("p t n -> p (t n)"))
         nc.sync.dma_start(out=offsets[:], in_=offs)
         nc.sync.dma_start(out=first[:], in_=s_rows[:, 0, :])
-        load_scale_rows(nc.sync, w2_bytes, w2_scales, range(4))
-        for c0, c1 in PIECES:
-            nc.sync.dma_start(out=planes[LAST][:, c0:c1], in_=s_rows[:, LAST, c0:c1])
+        load_scale_rows(nc.sync, w2_bytes, w2_scales, (0, 1, 2))
+        load_scale_rows(nc.sync, w1_bytes, w1_scales, (0, 1))
+        load_piece(0)
+        load_scale_rows(nc.sync, w1_bytes, w1_scales, (2,))
+        load_piece(1)
+        load_piece(2)
         load_queries(0)
+        load_scale_rows(nc.sync, w2_bytes, w2_scales, (3,))
+        load_scale_rows(nc.sync, w1_bytes, w1_scales, (3,))
         load_codes(w2_codes, w2_words)
         load_queries(1)
         load_codes(w1_codes, w1_words)
-        load_scale_rows(nc.sync, w1_bytes, w1_scales, range(4))
         for b in range(2, len(LOADS)):
             load_queries(b)
 
@@ -140,7 +146,7 @@ def tile_picked_recall_none_e_kernel(
             nc.tensor.matmul_mx(
                 out=acc[b][:],
                 lhsT=w_codes[:].bitcast(FP8X4),
-                lhsT_scale=w_bytes[:],
+                lhsT_scale=w_bytes[4:, :],
                 rhs=codes[:, j0:j1].bitcast(FP8X4),
                 rhs_scale=scale_bytes[:, j0:j1],
                 start=first,
@@ -176,16 +182,19 @@ def tile_picked_recall_none_e_kernel(
         gather(0, HALF, LAST)
         gather_rounded(HALF, S, LAST)
 
+        interleave(nc.vector.tensor_copy, 0, 128)
         quantize_memories(0, HALF)
         quantize_memories(HALF, S)
         for b in range(len(BLOCKS)):
             memories_times_w2(b)
-        interleave(nc.scalar.copy, 0, 256)
-        interleave(nc.vector.tensor_copy, 256, 384)
+        interleave(nc.scalar.copy, 128, 256)
+        interleave(nc.scalar.copy, 256, 384)
+        quantize_queries(*BLOCKS[0])
+        queries_times_w1(0)
         interleave(nc.vector.tensor_copy, 576, 768)
-        interleave(nc.scalar.copy, 384, 528)
-        interleave(nc.scalar.copy, 528, 576)
-        for b in (0, 1, 2):
+        interleave(nc.scalar.copy, 384, 512)
+        interleave(nc.scalar.copy, 512, 576)
+        for b in (1, 2):
             quantize_queries(*BLOCKS[b])
             queries_times_w1(b)
         interleave(nc.scalar.copy, 768, 896)

@@ -182,12 +182,12 @@ def tile_picked_recall_none_e_kernel(
         gather(0, HALF, LAST)
         gather_rounded(HALF, S, LAST)
 
-        interleave(nc.vector.tensor_copy, 0, 128)
+        interleave(nc.vector.tensor_copy, 0, 160)
         quantize_memories(0, HALF)
         quantize_memories(HALF, S)
         for b in range(len(BLOCKS)):
             memories_times_w2(b)
-        interleave(nc.scalar.copy, 128, 256)
+        interleave(nc.scalar.copy, 160, 256)
         interleave(nc.scalar.copy, 256, 384)
         quantize_queries(*BLOCKS[0])
         queries_times_w1(0)
@@ -198,12 +198,16 @@ def tile_picked_recall_none_e_kernel(
             quantize_queries(*BLOCKS[b])
             queries_times_w1(b)
         interleave(nc.scalar.copy, 768, 896)
-        interleave(nc.vector.tensor_copy, 896, S)
-        for b in (3, 4):
-            quantize_queries(*BLOCKS[b])
-            queries_times_w1(b)
-        for b in range(3):
+        interleave(nc.vector.tensor_copy, 896, 960)
+        interleave(nc.vector.tensor_copy, 960, S)
+        quantize_queries(*BLOCKS[3])
+        queries_times_w1(3)
+        quantize_queries(896, 960)
+        quantize_queries(960, S)
+        queries_times_w1(4)
+        for b in range(2):
             take_out_and_store(nc.scalar.copy, b)
+        take_out_and_store(nc.vector.tensor_copy, 2)
         for b in (3, 4):
             nc.vector.tensor_copy(out=result[b], in_=acc[b][:])
         nc.sync.dma_start(out=out[:, BLOCKS[3][0] :], in_=tail[:])

@@ -18,14 +18,11 @@ M = 128
 LISTED = 16
 LAST = PACK - 1
 HALF = S // 2
+QUARTER = S // 4
+SCALAR_PLACES = 128
 
-PIECES = ((0, 2432), (2432, 3776), (3776, T))
-SCALAR_ROUNDS = (1408, 256, 320)
-VECTOR_ROUNDS = 1536
 BLOCKS = ((0, 256), (256, 512), (512, 768), (768, 896), (896, S))
 LOADS = ((0, 384), (384, 768), (768, 896), (896, S))
-
-X_TILES = LOADS
 
 FLOPS = 2 * 2 * 512 * M * S
 
@@ -48,66 +45,57 @@ def tile_picked_recall_none_e_kernel(
         offsets = keep.tile([P, S // LISTED], U16)
         w1_codes = keep.tile([P, M], U32, align_bytes=256)
         w2_codes = keep.tile([P, M], U32, align_bytes=256)
-        x_tiles = [
-            keep.tile([P, PACK, j1 - j0], F32, name=f"x_raw{j0}", align_bytes=256) for j0, j1 in X_TILES
+        x_tiles = [keep.tile([P, PACK, j1 - j0], F32, name=f"x_raw{j0}", align_bytes=256)[:] for j0, j1 in LOADS[:2]]
+        x_tail = keep.tile([P, 2 * PACK * M], F32, align_bytes=256)
+        x_tiles = x_tiles + [
+            x_tail[:, i * PACK * M : (i + 1) * PACK * M].rearrange("p (t n) -> p t n", t=PACK) for i in range(2)
         ]
+        picked = keep.tile([P, S], BF16, align_bytes=64)
+        picked_wide = keep.tile([P, S], F32, align_bytes=64)
         s_packed = keep.tile([P, S * PACK], BF16, align_bytes=64)
-        rounded = keep.tile([P, T], BF16)
         s_codes = keep.tile([P, S], U32, align_bytes=64)
-        s_bytes = keep.tile([P, S], U8, align_bytes=64)
+        s_bytes = keep.tile([P, S], U8, align_bytes=256)
+        w1_bytes = s_bytes[:, HALF : HALF + M]
+        w2_bytes = s_bytes[:, :M]
         x_packed = keep.tile([P, S * PACK], BF16, align_bytes=256)
         x_codes = keep.tile([P, S], U32, align_bytes=64)
         x_bytes = keep.tile([P, S], U8, align_bytes=64)
+        tail = keep.tile([P, 2 * M], F32, align_bytes=256)
+        result = [x_tail[:, j0:j1] for j0, j1 in BLOCKS[:3]] + [tail[:, :M], tail[:, M:]]
         acc = [psum.tile([P, j1 - j0], F32, name=f"acc{b}") for b, (j0, j1) in enumerate(BLOCKS)]
 
-        raw2 = x_tiles[2][:].rearrange("p t n -> p (t n)")
-        wide = BLOCKS[0][1]
-        tail = keep.tile([P, wide], F32, align_bytes=256)
-        raw3 = x_tiles[3][:].rearrange("p t n -> p (t n)")
-        result = [raw2[:, :wide], raw2[:, wide:], raw3[:, :wide], tail[:, : wide // 2], tail[:, wide // 2 :]]
-
-        w1_bytes = s_bytes[:, HALF : HALF + M]
-        w2_bytes = s_bytes[:, :M]
-
         def raw_queries(j0, j1):
-            (first,) = [i for i, (lo, hi) in enumerate(X_TILES) if lo <= j0 and j1 <= hi]
-            return x_tiles[first][:, :, j0 - X_TILES[first][0] : j1 - X_TILES[first][0]]
+            (i,) = [i for i, (lo, hi) in enumerate(LOADS) if lo <= j0 and j1 <= hi]
+            return x_tiles[i][:, :, j0 - LOADS[i][0] : j1 - LOADS[i][0]]
 
         def load_codes(codes, words):
             nc.sync.dma_start(out=codes[:].bitcast(I32), in_=words[0].rearrange("p m r -> p (m r)").bitcast(I32))
 
-        def load_scale_rows(queue, tile, scales, quadrants):
+        def load_scale_rows(tile, scales, quadrants):
             for q in quadrants:
-                queue.dma_start(
+                nc.sync.dma_start(
                     out=tile[32 * q + 4 : 32 * q + 8, :].bitcast(I32),
                     in_=scales[0, 4 * q : 4 * q + 4, :].bitcast(I32),
                 )
 
         def load_queries(b):
             j0, j1 = LOADS[b]
-            nc.sync.dma_start(out=raw_queries(j0, j1), in_=x_rows[:, :, j0:j1])
-
-        def load_piece(i):
-            c0, c1 = PIECES[i]
-            nc.sync.dma_start(out=planes[LAST][:, c0:c1], in_=s_rows[:, LAST, c0:c1])
+            nc.sync.dma_start(out=x_tiles[b], in_=x_rows[:, :, j0:j1])
 
         nc.sync.dma_start(out=middle[:], in_=s_rows[:, 1:LAST, :].rearrange("p t n -> p (t n)"))
         nc.sync.dma_start(out=offsets[:], in_=offs)
         nc.sync.dma_start(out=first[:], in_=s_rows[:, 0, :])
-        load_scale_rows(nc.sync, w2_bytes, w2_scales, (0, 1, 2))
-        load_scale_rows(nc.sync, w1_bytes, w1_scales, (0, 1))
-        load_piece(0)
-        load_scale_rows(nc.sync, w1_bytes, w1_scales, (2,))
-        load_piece(1)
-        load_piece(2)
+        load_scale_rows(w2_bytes, w2_scales, (0, 1, 2))
+        load_scale_rows(w1_bytes, w1_scales, (0, 1))
+        nc.sync.dma_start(out=last[:], in_=s_rows[:, LAST, :])
         load_queries(0)
-        load_scale_rows(nc.sync, w2_bytes, w2_scales, (3,))
-        load_scale_rows(nc.sync, w1_bytes, w1_scales, (3,))
+        load_scale_rows(w2_bytes, w2_scales, (3,))
+        load_scale_rows(w1_bytes, w1_scales, (2, 3))
         load_codes(w2_codes, w2_words)
         load_queries(1)
         load_codes(w1_codes, w1_words)
-        for b in range(2, len(LOADS)):
-            load_queries(b)
+        load_queries(2)
+        load_queries(3)
 
         def slot(j0, j1, t):
             return s_packed[:, j0 * PACK : j1 * PACK].rearrange("p (n t) -> p n t", t=PACK)[:, :, t]
@@ -115,18 +103,18 @@ def tile_picked_recall_none_e_kernel(
         def entries(j0, j1):
             return offsets[:, j0 // LISTED : j1 // LISTED]
 
-        def gather(j0, j1, t):
+        def gather_into_place(j0, j1, t):
             nc.vector.tensor_copy(out=slot(j0, j1, t), in_=planes[t].indirect(entries(j0, j1)))
 
-        def round_columns(copy, t, c0, c1):
-            copy(out=rounded[:, c0:c1], in_=planes[t][:, c0:c1])
-
-        def gather_rounded(j0, j1, t):
+        def gather_side_by_side(tile, j0, j1, t):
             nc.scalar.activation(
-                out=slot(j0, j1, t),
-                in_=rounded[:].indirect(entries(j0, j1)),
+                out=tile[:, j0:j1],
+                in_=planes[t].indirect(entries(j0, j1)),
                 func=mybir.ActivationFunctionType.Copy,
             )
+
+        def place(copy, tile, j0, j1, t):
+            copy(out=slot(j0, j1, t), in_=tile[:, j0:j1])
 
         def interleave(copy, j0, j1):
             copy(
@@ -141,7 +129,7 @@ def tile_picked_recall_none_e_kernel(
                 in_=packed[:, j0 * PACK : j1 * PACK],
             )
 
-        def multiply(b, w_codes, w_bytes, codes, scale_bytes, first):
+        def multiply(b, w_codes, w_bytes, codes, scale_bytes, opens):
             j0, j1 = BLOCKS[b]
             nc.tensor.matmul_mx(
                 out=acc[b][:],
@@ -149,51 +137,44 @@ def tile_picked_recall_none_e_kernel(
                 lhsT_scale=w_bytes[4:, :],
                 rhs=codes[:, j0:j1].bitcast(FP8X4),
                 rhs_scale=scale_bytes[:, j0:j1],
-                start=first,
-                stop=not first,
+                start=opens,
+                stop=not opens,
             )
-
-        def quantize_memories(j0, j1):
-            quantize(s_packed, s_codes, s_bytes, j0, j1)
 
         def quantize_queries(j0, j1):
             quantize(x_packed, x_codes, x_bytes, j0, j1)
 
-        def memories_times_w2(b):
-            multiply(b, w2_codes, w2_bytes, s_codes, s_bytes, True)
-
         def queries_times_w1(b):
             multiply(b, w1_codes, w1_bytes, x_codes, x_bytes, False)
 
-        def take_out_and_store(copy, b):
+        def take_out(copy, b):
             j0, j1 = BLOCKS[b]
             copy(out=result[b], in_=acc[b][:])
             nc.sync.dma_start(out=out[:, j0:j1], in_=result[b])
 
-        round_columns(nc.vector.tensor_copy, 2, 0, VECTOR_ROUNDS)
-        round_columns(nc.scalar.copy, 2, VECTOR_ROUNDS, T)
-        gather(0, S, 1)
-        gather_rounded(0, S, 2)
-        gather(0, S, 0)
-        for (c0, c1), share in zip(PIECES, SCALAR_ROUNDS):
-            round_columns(nc.scalar.copy, LAST, c0, c0 + share)
-            if c0 + share < c1:
-                round_columns(nc.vector.tensor_copy, LAST, c0 + share, c1)
-        gather(0, HALF, LAST)
-        gather_rounded(HALF, S, LAST)
-
-        interleave(nc.vector.tensor_copy, 0, 160)
-        quantize_memories(0, HALF)
-        quantize_memories(HALF, S)
+        gather_into_place(0, S, 1)
+        gather_side_by_side(picked_wide, 0, S, 2)
+        place(nc.vector.tensor_copy, picked_wide, 0, S, 2)
+        gather_into_place(0, HALF, 0)
+        gather_side_by_side(picked, HALF, S, 0)
+        place(nc.vector.tensor_copy, picked, HALF, S, 0)
+        gather_into_place(0, HALF, LAST)
+        gather_side_by_side(picked, HALF, HALF + QUARTER, LAST)
+        gather_side_by_side(picked, HALF + QUARTER, S, LAST)
+        place(nc.scalar.copy, picked, HALF, HALF + SCALAR_PLACES, LAST)
+        place(nc.vector.tensor_copy, picked, HALF + SCALAR_PLACES, S, LAST)
+        quantize(s_packed, s_codes, s_bytes, 0, HALF)
+        quantize(s_packed, s_codes, s_bytes, HALF, S)
         for b in range(len(BLOCKS)):
-            memories_times_w2(b)
-        interleave(nc.scalar.copy, 160, 256)
+            multiply(b, w2_codes, w2_bytes, s_codes, s_bytes, True)
+
+        interleave(nc.scalar.copy, 0, 256)
         interleave(nc.scalar.copy, 256, 384)
         quantize_queries(*BLOCKS[0])
         queries_times_w1(0)
-        interleave(nc.vector.tensor_copy, 576, 768)
+        interleave(nc.vector.tensor_copy, 528, 768)
         interleave(nc.scalar.copy, 384, 512)
-        interleave(nc.scalar.copy, 512, 576)
+        interleave(nc.scalar.copy, 512, 528)
         for b in (1, 2):
             quantize_queries(*BLOCKS[b])
             queries_times_w1(b)
@@ -206,8 +187,6 @@ def tile_picked_recall_none_e_kernel(
         quantize_queries(960, S)
         queries_times_w1(4)
         for b in range(2):
-            take_out_and_store(nc.scalar.copy, b)
-        take_out_and_store(nc.vector.tensor_copy, 2)
-        for b in (3, 4):
-            nc.vector.tensor_copy(out=result[b], in_=acc[b][:])
-        nc.sync.dma_start(out=out[:, BLOCKS[3][0] :], in_=tail[:])
+            take_out(nc.scalar.copy, b)
+        for b in range(2, len(BLOCKS)):
+            take_out(nc.vector.tensor_copy, b)

@@ -19,10 +19,10 @@ LISTED = 16
 LAST = PACK - 1
 HALF = S // 2
 QUARTER = S // 4
-SCALAR_PLACES = 128
 
 BLOCKS = ((0, 256), (256, 512), (512, 768), (768, 896), (896, S))
-LOADS = ((0, 384), (384, 768), (768, 896), (896, S))
+LOADS = BLOCKS
+X_TILES = ((0, 256), (256, 768), (768, 896), (896, S))
 
 FLOPS = 2 * 2 * 512 * M * S
 
@@ -45,7 +45,7 @@ def tile_picked_recall_none_e_kernel(
         offsets = keep.tile([P, S // LISTED], U16)
         w1_codes = keep.tile([P, M], U32, align_bytes=256)
         w2_codes = keep.tile([P, M], U32, align_bytes=256)
-        x_tiles = [keep.tile([P, PACK, j1 - j0], F32, name=f"x_raw{j0}", align_bytes=256)[:] for j0, j1 in LOADS[:2]]
+        x_tiles = [keep.tile([P, PACK, j1 - j0], F32, name=f"x_raw{j0}", align_bytes=256)[:] for j0, j1 in X_TILES[:2]]
         x_tail = keep.tile([P, 2 * PACK * M], F32, align_bytes=256)
         x_tiles = x_tiles + [
             x_tail[:, i * PACK * M : (i + 1) * PACK * M].rearrange("p (t n) -> p t n", t=PACK) for i in range(2)
@@ -65,8 +65,8 @@ def tile_picked_recall_none_e_kernel(
         acc = [psum.tile([P, j1 - j0], F32, name=f"acc{b}") for b, (j0, j1) in enumerate(BLOCKS)]
 
         def raw_queries(j0, j1):
-            (i,) = [i for i, (lo, hi) in enumerate(LOADS) if lo <= j0 and j1 <= hi]
-            return x_tiles[i][:, :, j0 - LOADS[i][0] : j1 - LOADS[i][0]]
+            (i,) = [i for i, (lo, hi) in enumerate(X_TILES) if lo <= j0 and j1 <= hi]
+            return x_tiles[i][:, :, j0 - X_TILES[i][0] : j1 - X_TILES[i][0]]
 
         def load_codes(codes, words):
             nc.sync.dma_start(out=codes[:].bitcast(I32), in_=words[0].rearrange("p m r -> p (m r)").bitcast(I32))
@@ -80,7 +80,7 @@ def tile_picked_recall_none_e_kernel(
 
         def load_queries(b):
             j0, j1 = LOADS[b]
-            nc.sync.dma_start(out=x_tiles[b], in_=x_rows[:, :, j0:j1])
+            nc.sync.dma_start(out=raw_queries(j0, j1), in_=x_rows[:, :, j0:j1])
 
         nc.sync.dma_start(out=middle[:], in_=s_rows[:, 1:LAST, :].rearrange("p t n -> p (t n)"))
         nc.sync.dma_start(out=offsets[:], in_=offs)
@@ -94,8 +94,8 @@ def tile_picked_recall_none_e_kernel(
         load_codes(w2_codes, w2_words)
         load_queries(1)
         load_codes(w1_codes, w1_words)
-        load_queries(2)
-        load_queries(3)
+        for b in range(2, len(LOADS)):
+            load_queries(b)
 
         def slot(j0, j1, t):
             return s_packed[:, j0 * PACK : j1 * PACK].rearrange("p (n t) -> p n t", t=PACK)[:, :, t]
@@ -153,28 +153,26 @@ def tile_picked_recall_none_e_kernel(
             nc.sync.dma_start(out=out[:, j0:j1], in_=result[b])
 
         gather_into_place(0, S, 1)
-        gather_side_by_side(picked_wide, 0, S, 2)
-        place(nc.vector.tensor_copy, picked_wide, 0, S, 2)
-        gather_into_place(0, HALF, 0)
-        gather_side_by_side(picked, HALF, S, 0)
-        place(nc.vector.tensor_copy, picked, HALF, S, 0)
+        gather_side_by_side(picked_wide, 0, HALF, 2)
+        gather_side_by_side(picked_wide, HALF, S, 2)
+        place(nc.vector.tensor_copy, picked_wide, 0, HALF, 2)
+        place(nc.scalar.copy, picked_wide, HALF, S, 2)
+        gather_into_place(0, S, 0)
         gather_into_place(0, HALF, LAST)
-        gather_side_by_side(picked, HALF, HALF + QUARTER, LAST)
-        gather_side_by_side(picked, HALF + QUARTER, S, LAST)
-        place(nc.scalar.copy, picked, HALF, HALF + SCALAR_PLACES, LAST)
-        place(nc.vector.tensor_copy, picked, HALF + SCALAR_PLACES, S, LAST)
+        for j0 in (HALF, HALF + QUARTER):
+            gather_side_by_side(picked, j0, j0 + QUARTER, LAST)
+            place(nc.vector.tensor_copy, picked, j0, j0 + QUARTER, LAST)
         quantize(s_packed, s_codes, s_bytes, 0, HALF)
         quantize(s_packed, s_codes, s_bytes, HALF, S)
         for b in range(len(BLOCKS)):
             multiply(b, w2_codes, w2_bytes, s_codes, s_bytes, True)
 
         interleave(nc.scalar.copy, 0, 256)
-        interleave(nc.scalar.copy, 256, 384)
         quantize_queries(*BLOCKS[0])
         queries_times_w1(0)
-        interleave(nc.vector.tensor_copy, 528, 768)
-        interleave(nc.scalar.copy, 384, 512)
-        interleave(nc.scalar.copy, 512, 528)
+        interleave(nc.scalar.copy, 256, 496)
+        interleave(nc.vector.tensor_copy, 576, 768)
+        interleave(nc.scalar.copy, 496, 576)
         for b in (1, 2):
             quantize_queries(*BLOCKS[b])
             queries_times_w1(b)

@@ -157,11 +157,22 @@ def tile_picked_recall_none_e_kernel(
         gather_side_by_side(picked_wide, HALF, S, 2)
         place(nc.vector.tensor_copy, picked_wide, 0, HALF, 2)
         place(nc.scalar.copy, picked_wide, HALF, S, 2)
-        gather_into_place(0, S, 0)
+        gather_into_place(0, S - QUARTER, 0)
+        gather_side_by_side(picked, S - QUARTER, S, 0)
+        place(nc.vector.tensor_copy, picked, S - QUARTER, S, 0)
         gather_into_place(0, HALF, LAST)
-        for j0 in (HALF, HALF + QUARTER):
-            gather_side_by_side(picked, j0, j0 + QUARTER, LAST)
-            place(nc.vector.tensor_copy, picked, j0, j0 + QUARTER, LAST)
+        for j0 in (S - QUARTER, S - M):
+            gather_side_by_side(picked, j0, j0 + M, LAST)
+            nc.gpsimd.tensor_scalar(
+                out=slot(j0, j0 + M, LAST),
+                in0=picked[:, j0 : j0 + M],
+                scalar1=1.0,
+                scalar2=0.0,
+                op0=mybir.AluOpType.mult,
+                op1=mybir.AluOpType.add,
+            )
+        gather_side_by_side(picked, HALF, S - QUARTER, LAST)
+        place(nc.vector.tensor_copy, picked, HALF, S - QUARTER, LAST)
         quantize(s_packed, s_codes, s_bytes, 0, HALF)
         quantize(s_packed, s_codes, s_bytes, HALF, S)
         for b in range(len(BLOCKS)):

@@ -61,7 +61,8 @@ def tile_picked_recall_none_e_kernel(
         x_codes = keep.tile([P, S], U32, align_bytes=64)
         x_bytes = keep.tile([P, S], U8, align_bytes=64)
         tail = keep.tile([P, 2 * M], F32, align_bytes=256)
-        result = [x_tail[:, j0:j1] for j0, j1 in BLOCKS[:3]] + [tail[:, :M], tail[:, M:]]
+        spent = x_packed[:, BLOCKS[1][0] * PACK : BLOCKS[1][1] * PACK].bitcast(F32)
+        result = [spent[:, : 2 * M], spent[:, 2 * M :], x_tail[:, 512:768], tail[:, :M], tail[:, M:]]
         acc = [psum.tile([P, j1 - j0], F32, name=f"acc{b}") for b, (j0, j1) in enumerate(BLOCKS)]
 
         def raw_queries(j0, j1):
@@ -86,11 +87,11 @@ def tile_picked_recall_none_e_kernel(
         nc.sync.dma_start(out=offsets[:], in_=offs)
         nc.sync.dma_start(out=first[:], in_=s_rows[:, 0, :])
         load_scale_rows(w2_bytes, w2_scales, (0, 1, 2))
-        load_scale_rows(w1_bytes, w1_scales, (0, 1))
+        load_scale_rows(w1_bytes, w1_scales, (0, 1, 2))
         nc.sync.dma_start(out=last[:], in_=s_rows[:, LAST, :])
         load_queries(0)
         load_scale_rows(w2_bytes, w2_scales, (3,))
-        load_scale_rows(w1_bytes, w1_scales, (2, 3))
+        load_scale_rows(w1_bytes, w1_scales, (3,))
         load_codes(w2_codes, w2_words)
         load_queries(1)
         load_codes(w1_codes, w1_words)

from contextlib import ExitStack

import concourse.mybir as mybir

F32 = mybir.dt.float32
BF16 = mybir.dt.bfloat16
I32 = mybir.dt.int32
U32 = mybir.dt.uint32
U16 = mybir.dt.uint16
U8 = mybir.dt.uint8
FP8X4 = mybir.dt.float8_e4m3fn_x4

P = 128
PACK = 4
T = 4096
S = 1024
M = 128
LISTED = 16
LAST = PACK - 1
HALF = S // 2
QUARTER = S // 4

BLOCKS = ((0, 256), (256, 512), (512, 768), (768, 896), (896, S))
LOADS = BLOCKS
X_TILES = ((0, 256), (256, 768), (768, 896), (896, S))

FLOPS = 2 * 2 * 512 * M * S


def tile_picked_recall_none_e_kernel(
    tc, xT, sT, w1_words, w1_scales, w2_words, w2_scales, offs, out
):
    nc = tc.nc
    with ExitStack() as ctx:
        keep = ctx.enter_context(tc.tile_pool(name="keep", bufs=1))
        psum = ctx.enter_context(tc.psum_pool(name="psum", bufs=1))

        s_rows = sT.rearrange("(p t) n -> p t n", t=PACK)
        x_rows = xT.rearrange("(p t) n -> p t n", t=PACK)

        middle = keep.tile([P, 2 * T], F32, align_bytes=256)
        first = keep.tile([P, T], F32, align_bytes=256)
        last = keep.tile([P, T], F32, align_bytes=256)
        planes = [first[:], middle[:, :T], middle[:, T:], last[:]]
        offsets = keep.tile([P, S // LISTED], U16)
        w1_codes = keep.tile([P, M], U32, align_bytes=256)
        w2_codes = keep.tile([P, M], U32, align_bytes=256)
        x_tiles = [keep.tile([P, PACK, j1 - j0], F32, name=f"x_raw{j0}", align_bytes=256)[:] for j0, j1 in X_TILES[:2]]
        x_tail = keep.tile([P, 2 * PACK * M], F32, align_bytes=256)
        x_tiles = x_tiles + [
            x_tail[:, i * PACK * M : (i + 1) * PACK * M].rearrange("p (t n) -> p t n", t=PACK) for i in range(2)
        ]
        picked = keep.tile([P, S], BF16, align_bytes=64)
        picked_wide = keep.tile([P, S], F32, align_bytes=64)
        s_packed = keep.tile([P, S * PACK], BF16, align_bytes=64)
        s_codes = keep.tile([P, S], U32, align_bytes=64)
        s_bytes = keep.tile([P, S], U8, align_bytes=256)
        w1_bytes = s_bytes[:, HALF : HALF + M]
        w2_bytes = s_bytes[:, :M]
        x_packed = keep.tile([P, S * PACK], BF16, align_bytes=256)
        x_codes = keep.tile([P, S], U32, align_bytes=64)
        x_bytes = keep.tile([P, S], U8, align_bytes=64)
        tail = keep.tile([P, 2 * M], F32, align_bytes=256)
        spent = x_packed[:, BLOCKS[1][0] * PACK : BLOCKS[1][1] * PACK].bitcast(F32)
        result = [spent[:, : 2 * M], spent[:, 2 * M :], x_tail[:, 512:768], tail[:, :M], tail[:, M:]]
        acc = [psum.tile([P, j1 - j0], F32, name=f"acc{b}") for b, (j0, j1) in enumerate(BLOCKS)]

        def raw_queries(j0, j1):
            (i,) = [i for i, (lo, hi) in enumerate(X_TILES) if lo <= j0 and j1 <= hi]
            return x_tiles[i][:, :, j0 - X_TILES[i][0] : j1 - X_TILES[i][0]]

        def load_codes(codes, words):
            nc.sync.dma_start(out=codes[:].bitcast(I32), in_=words[0].rearrange("p m r -> p (m r)").bitcast(I32))

        def load_scale_rows(tile, scales, quadrants):
            for q in quadrants:
                nc.sync.dma_start(
                    out=tile[32 * q + 4 : 32 * q + 8, :].bitcast(I32),
                    in_=scales[0, 4 * q : 4 * q + 4, :].bitcast(I32),
                )

        def load_queries(b):
            j0, j1 = LOADS[b]
            nc.sync.dma_start(out=raw_queries(j0, j1), in_=x_rows[:, :, j0:j1])

        nc.sync.dma_start(out=middle[:], in_=s_rows[:, 1:LAST, :].rearrange("p t n -> p (t n)"))
        nc.sync.dma_start(out=offsets[:], in_=offs)
        nc.sync.dma_start(out=first[:], in_=s_rows[:, 0, :])
        load_scale_rows(w2_bytes, w2_scales, (0, 1, 2))
        load_scale_rows(w1_bytes, w1_scales, (0, 1, 2))
        nc.sync.dma_start(out=last[:], in_=s_rows[:, LAST, :])
        load_queries(0)
        load_scale_rows(w2_bytes, w2_scales, (3,))
        load_scale_rows(w1_bytes, w1_scales, (3,))
        load_codes(w2_codes, w2_words)
        load_queries(1)
        load_codes(w1_codes, w1_words)
        for b in range(2, len(LOADS)):
            load_queries(b)

        def slot(j0, j1, t):
            return s_packed[:, j0 * PACK : j1 * PACK].rearrange("p (n t) -> p n t", t=PACK)[:, :, t]

        def entries(j0, j1):
            return offsets[:, j0 // LISTED : j1 // LISTED]

        def gather_into_place(j0, j1, t):
            nc.vector.tensor_copy(out=slot(j0, j1, t), in_=planes[t].indirect(entries(j0, j1)))

        def gather_side_by_side(tile, j0, j1, t):
            nc.scalar.activation(
                out=tile[:, j0:j1],
                in_=planes[t].indirect(entries(j0, j1)),
                func=mybir.ActivationFunctionType.Copy,
            )

        def place(copy, tile, j0, j1, t):
            copy(out=slot(j0, j1, t), in_=tile[:, j0:j1])

        def interleave(copy, j0, j1):
            copy(
                out=x_packed[:, j0 * PACK : j1 * PACK].rearrange("p (c i t) -> p c t i", i=4, t=PACK),
                in_=raw_queries(j0, j1).rearrange("p t (c i) -> p c t i", i=4),
            )

        def quantize(packed, codes, scale_bytes, j0, j1):
            nc.vector.quantize_mx(
                out=codes[:, j0:j1].bitcast(FP8X4),
                scales=scale_bytes[:, j0:j1],
                in_=packed[:, j0 * PACK : j1 * PACK],
            )

        def multiply(b, w_codes, w_bytes, codes, scale_bytes, opens):
            j0, j1 = BLOCKS[b]
            nc.tensor.matmul_mx(
                out=acc[b][:],
                lhsT=w_codes[:].bitcast(FP8X4),
                lhsT_scale=w_bytes[4:, :],
                rhs=codes[:, j0:j1].bitcast(FP8X4),
                rhs_scale=scale_bytes[:, j0:j1],
                start=opens,
                stop=not opens,
            )

        def quantize_queries(j0, j1):
            quantize(x_packed, x_codes, x_bytes, j0, j1)

        def queries_times_w1(b):
            multiply(b, w1_codes, w1_bytes, x_codes, x_bytes, False)

        def take_out(copy, b):
            j0, j1 = BLOCKS[b]
            copy(out=result[b], in_=acc[b][:])
            nc.sync.dma_start(out=out[:, j0:j1], in_=result[b])

        gather_into_place(0, S, 1)
        gather_side_by_side(picked_wide, 0, HALF, 2)
        gather_side_by_side(picked_wide, HALF, S, 2)
        place(nc.vector.tensor_copy, picked_wide, 0, HALF, 2)
        place(nc.scalar.copy, picked_wide, HALF, S, 2)
        gather_into_place(0, S - QUARTER, 0)
        gather_side_by_side(picked, S - QUARTER, S, 0)
        place(nc.vector.tensor_copy, picked, S - QUARTER, S, 0)
        gather_into_place(0, HALF, LAST)
        for j0 in (S - QUARTER, S - M):
            gather_side_by_side(picked, j0, j0 + M, LAST)
            nc.gpsimd.tensor_scalar(
                out=slot(j0, j0 + M, LAST),
                in0=picked[:, j0 : j0 + M],
                scalar1=1.0,
                scalar2=0.0,
                op0=mybir.AluOpType.mult,
                op1=mybir.AluOpType.add,
            )
        gather_side_by_side(picked, HALF, S - QUARTER, LAST)
        place(nc.vector.tensor_copy, picked, HALF, S - QUARTER, LAST)
        quantize(s_packed, s_codes, s_bytes, 0, HALF)
        quantize(s_packed, s_codes, s_bytes, HALF, S)
        for b in range(len(BLOCKS)):
            multiply(b, w2_codes, w2_bytes, s_codes, s_bytes, True)

        interleave(nc.scalar.copy, 0, 256)
        quantize_queries(*BLOCKS[0])
        queries_times_w1(0)
        interleave(nc.scalar.copy, 256, 496)
        interleave(nc.vector.tensor_copy, 576, 768)
        interleave(nc.scalar.copy, 496, 576)
        for b in (1, 2):
            quantize_queries(*BLOCKS[b])
            queries_times_w1(b)
        interleave(nc.scalar.copy, 768, 896)
        interleave(nc.vector.tensor_copy, 896, 960)
        interleave(nc.vector.tensor_copy, 960, S)
        quantize_queries(*BLOCKS[3])
        queries_times_w1(3)
        quantize_queries(896, 960)
        quantize_queries(960, S)
        queries_times_w1(4)
        for b in range(2):
            take_out(nc.scalar.copy, b)
        for b in range(2, len(BLOCKS)):
            take_out(nc.vector.tensor_copy, b)
